import numpy as np
import ml_dtypes


def mxq(x, axis, fmt="e4m3"):
    dtype, down = {"e4m3": (ml_dtypes.float8_e4m3fn, 7), "e5m2": (ml_dtypes.float8_e5m2, 14)}[fmt]
    v = np.moveaxis(np.asarray(x, np.float32).astype(ml_dtypes.bfloat16).astype(np.float64), axis, -1)
    blocks = v.reshape(v.shape[:-1] + (-1, 32))
    amax = np.abs(blocks).max(-1, keepdims=True)
    byte = np.maximum(np.where(amax > 0, np.frexp(amax)[1] - 1 + 127, 0) - down, 1)
    scale = np.exp2(byte - 127.0)
    codes = (blocks / scale).astype(np.float32).astype(dtype).astype(np.float64)
    return np.moveaxis((codes * scale).reshape(v.shape), -1, axis)


WIDE = False


def mx_kscale(k):
    if not WIDE:
        return np.ones(k)
    levels = np.array([10, -10, 5, -5, 0])
    if k % 512:
        return np.exp2(np.random.permutation(np.resize(levels, k // 32))).repeat(32)
    a = np.empty((k // 512, 16))
    for p in range(k // 512):
        a[p, :8] = np.random.permutation(np.resize(levels, 8))
        for g in range(8):
            far = levels[np.abs(levels - a[p, g]) >= 10]
            a[p, g + 8] = far[np.random.randint(len(far))]
    return np.exp2(a.ravel()).repeat(32)


def f64(x):
    return np.asarray(x).astype(np.float64)


def striped(idx):
    return np.tile(idx.reshape(-1, 16).T, (8, 1)).astype(np.uint16)


def unstriped(offs):
    return offs[:16].T.reshape(-1).astype(np.int64)


def pack_weight(w):
    k, n = w.shape
    w = f64(np.asarray(w, np.float32).astype(ml_dtypes.bfloat16)).reshape(k // 32, 32, n)
    amax = np.abs(w).max(1)
    byte = np.clip(np.where(amax > 0, np.frexp(amax)[1] - 1 + 127 - 7, 1), 1, 254)
    scaled = (w * np.exp2(127.0 - byte)[:, None, :]).reshape(k, n).astype(np.float32)
    words = np.ascontiguousarray(scaled.reshape(k // 512, 128, 4, n).transpose(0, 1, 3, 2)).astype(ml_dtypes.float8_e4m3fn).view(np.uint8)
    return words, np.ascontiguousarray(byte.astype(np.uint8).reshape(k // 512, 16, n))


def unpack_weight(words, scales):
    g, p, n, _ = words.shape
    vals = np.ascontiguousarray(words).view(ml_dtypes.float8_e4m3fn).astype(np.float64) * np.repeat(np.exp2(scales.astype(np.float64) - 127.0), 8, axis=1)[..., None]
    return vals.transpose(0, 1, 3, 2).reshape(g * 512, n)


def gelu(v):
    return 0.5 * v * (1.0 + np.tanh(np.sqrt(2.0 / np.pi) * (v + 0.044715 * v**3)))


K, T, S, H, N, V = 1024, 2048, 512, 512, 256, 128


def setup_inputs():
    n = np.random.standard_normal
    s = mx_kscale(K)[:, None]
    u = mx_kscale(H)
    near = np.random.permutation(S)
    packed_xT = pack_weight(n((K, T)) * s)
    return {
        "x_words": packed_xT[0],
        "x_scales": packed_xT[1],
        "w1": (n((K, H)) / np.sqrt(K) / s * u).astype(np.float32),
        "w2": (n((H, N)) / np.sqrt(H) / u[:, None]).astype(np.float32),
        "offs": striped(np.random.permutation(T)[:S]),
        "give": striped(near[:V]),
        "take": striped(near[V : 2 * V]),
    }


def reference(x_words, x_scales, w1, w2, offs, give, take):
    xq = unpack_weight(x_words, x_scales)[:, unstriped(offs)]
    h = gelu(mxq(f64(w1), 0, "e4m3").T @ xq)
    z = h.copy()
    z[:, unstriped(take)] = h[:, unstriped(give)]
    return mxq(f64(w2), 0, "e4m3").T @ mxq(z, 0, "e4m3")

@@ -1,0 +1,176 @@
+from contextlib import ExitStack
+
+import concourse.mybir as mybir
+
+K, T, S, H, N, V = 1024, 2048, 512, 512, 256, 128
+FLOPS = 2 * K * H * S + 2 * H * N * S
+
+F32 = mybir.dt.float32
+BF16 = mybir.dt.bfloat16
+I32 = mybir.dt.int32
+U32 = mybir.dt.uint32
+U16 = mybir.dt.uint16
+U8 = mybir.dt.uint8
+FP8X4 = mybir.dt.float8_e4m3fn_x4
+GELU = mybir.ActivationFunctionType.Gelu_apprx_tanh
+
+P = 128
+PACK = 4
+K_PASS = P * PACK
+PASSES = K // K_PASS
+HALF = S // 2
+LIST_ROWS = 16
+
+
+def tile_picked_ycutmix_gelu_p_kernel(tc, x_words, x_scales, w1, w2, offs, give, take, out):
+    nc = tc.nc
+    with ExitStack() as ctx:
+        lists = ctx.enter_context(tc.tile_pool(name="lists", bufs=1))
+        keep = ctx.enter_context(tc.tile_pool(name="keep", bufs=1))
+        psum = ctx.enter_context(tc.psum_pool(name="psum", bufs=1))
+
+        def sb(name, shape, dtype, tag=None):
+            return keep.tile(shape, dtype, name=name, tag=tag or name, align_bytes=64)
+
+        halves = [slice(0, HALF), slice(HALF, S)]
+        whole = slice(0, S)
+
+        warm_in = sb("warm_in", [P, 8], F32)
+        warm_out = sb("warm_out", [P, 8], F32)
+        nc.vector.memset(warm_in[:], 0.0)
+        nc.scalar.activation(warm_out[:], warm_in[:], GELU)
+
+        scale_rows = sb("scale_rows", [P, T], U8)
+        nc.gpsimd.memset(scale_rows[:].bitcast(I32), 0)
+        for q in range(4):
+            nc.gpsimd.dma_start(
+                scale_rows[32 * q : 32 * q + 4 * PASSES, :].bitcast(I32),
+                x_scales[:, 4 * q : 4 * q + 4, :].bitcast(I32),
+            )
+
+        w1_raw = [sb(f"w1_raw{o}", [P, PACK, H], F32) for o in range(PASSES)]
+        x_tab = [sb(f"x_tab{o}", [P, T], U32) for o in range(PASSES)]
+        w2_raw = sb("w2_raw", [P, PACK, N], F32)
+        offs_sb = lists.tile([P, S // LIST_ROWS], U16, name="offs_sb")
+        give_sb = lists.tile([P, V // LIST_ROWS], U16, name="give_sb")
+        take_sb = lists.tile([P, V // LIST_ROWS], U16, name="take_sb")
+
+        for o in range(PASSES):
+            nc.sync.dma_start(w1_raw[o][:], w1[o * K_PASS : (o + 1) * K_PASS, :].rearrange("(p j) c -> p j c", j=PACK))
+            if o == 0:
+                nc.sync.dma_start(offs_sb[:], offs)
+        for o in range(PASSES):
+            nc.sync.dma_start(x_tab[o][:].bitcast(I32), x_words[o].rearrange("p c r -> p (c r)").bitcast(I32))
+        nc.sync.dma_start(w2_raw[:], w2.rearrange("(p j) n -> p j n", j=PACK))
+        nc.sync.dma_start(give_sb[:], give)
+        nc.sync.dma_start(take_sb[:], take)
+
+        w1_bf = [sb(f"w1_bf{o}", [P, H * PACK], BF16) for o in range(PASSES)]
+
+        def w1_views(o):
+            return (
+                w1_bf[o][:].rearrange("p (t m j) -> p m j t", t=PACK, j=PACK),
+                w1_raw[o][:].rearrange("p j (m t) -> p m j t", t=PACK),
+            )
+
+        def quantise(name, values, tag=None):
+            width = values.shape[1] // PACK
+            codes = sb(f"{name}_codes", [P, width], U32, tag=tag)
+            scales = sb(f"{name}_scales", [P, width], U8)
+            nc.vector.quantize_mx(out=codes[:].bitcast(FP8X4), scales=scales[:], in_=values)
+            return codes, scales
+
+        def pick_words(o, tag):
+            picked = sb(f"x_codes{o}", [P, S], U32, tag=tag)
+            half_cols = HALF // LIST_ROWS
+            for a in range(2):
+                nc.vector.tensor_copy(picked[:, halves[a]], x_tab[o][:].indirect(offs_sb[:, a * half_cols : (a + 1) * half_cols]))
+            return picked
+
+        pieces = [(0, halves[0]), (1, halves[0]), (0, halves[1]), (1, halves[1]), (2, whole), (3, whole)]
+        acc = [psum.tile([P, cols.stop - cols.start], F32, name=f"acc{i}", tag=f"bank{i}") for i, (t, cols) in enumerate(pieces)]
+
+        def first_product(o, w_codes, w_scales, x_codes):
+            for i, (t, cols) in enumerate(pieces):
+                nc.tensor.matmul_mx(
+                    out=acc[i][:],
+                    lhsT=w_codes[:, t * P : (t + 1) * P].bitcast(FP8X4),
+                    lhsT_scale=w_scales[:, t * P : (t + 1) * P],
+                    rhs=x_codes[:, cols].bitcast(FP8X4),
+                    rhs_scale=x_scale[4 * o : P, cols],
+                    start=(o == 0),
+                    stop=(o == PASSES - 1),
+                )
+
+        nc.vector.tensor_copy(*w1_views(0))
+        nc.scalar.copy(*w1_views(1))
+        w1_mx0 = quantise("w1_0", w1_bf[0][:])
+        x_scale = sb("x_scale", [P, S], U8)
+        nc.vector.tensor_copy(x_scale[:], scale_rows[:].indirect(offs_sb[:]))
+        x_codes0 = pick_words(0, "scale_rows")
+        first_product(0, *w1_mx0, x_codes0)
+        w1_mx1 = quantise("w1_1", w1_bf[1][:], tag="x_tab0")
+        x_codes1 = pick_words(1, "w1_bf1")
+        first_product(1, *w1_mx1, x_codes1)
+
+        w2_bf = sb("w2_bf", [P, N * PACK], BF16, tag="x_tab1")
+        nc.vector.tensor_copy(
+            w2_bf[:].rearrange("p (c i j) -> p c j i", i=PACK, j=PACK),
+            w2_raw[:].rearrange("p j (c i) -> p c j i", i=PACK),
+        )
+
+        z = [sb(f"z{t}", [P, S], F32) for t in range(PACK)]
+        given = [sb(f"given{t}", [P, V], F32) for t in range(PACK)]
+        for i, (t, cols) in enumerate(pieces):
+            nc.scalar.activation(z[t][:, cols], acc[i][:], GELU)
+
+        def fetch(t):
+            nc.vector.tensor_copy(given[t][:], z[t][:].indirect(give_sb[:]))
+
+        def put(t):
+            nc.vector.tensor_copy(z[t][:].indirect(take_sb[:]), given[t][:])
+
+        fetch(0)
+        for t in range(PACK):
+            if t + 1 < PACK:
+                fetch(t + 1)
+            put(t)
+
+        pairs = [sb(f"pairs{a}", [P, HALF * PACK], BF16) for a in range(2)]
+        for t in range(PACK):
+            for a in range(2):
+                dst = pairs[a][:].rearrange("p (u c e) -> p u c e", u=2, e=2)[:, t // 2, :, t % 2]
+                if t >= 2 and a == 0:
+                    nc.vector.tensor_copy(dst, z[t][:, halves[a]])
+                else:
+                    nc.scalar.copy(dst, z[t][:, halves[a]])
+        w2_codes, w2_scales = quantise("w2", w2_bf[:], tag="given3")
+
+        z_bf = [sb(f"z_bf{a}", [P, HALF * PACK], BF16) for a in range(2)]
+        nc.vector.tensor_copy(
+            z_bf[0][:].bitcast(I32).rearrange("p (c u) -> p c u", u=2),
+            pairs[0][:].bitcast(I32).rearrange("p (u c) -> p c u", u=2),
+        )
+        nc.scalar.copy(
+            z_bf[1][:].bitcast(U32).rearrange("p (c u) -> p c u", u=2),
+            pairs[1][:].bitcast(U32).rearrange("p (u c) -> p c u", u=2),
+        )
+        z_mx = [quantise(f"z{a}", z_bf[a][:]) for a in range(2)]
+        for a in range(2):
+            for m in range(N // P):
+                res = psum.tile([P, HALF], F32, name=f"res{a}_{m}", tag=f"bank{2 * a + m}")
+                nc.tensor.matmul_mx(
+                    out=res[:],
+                    lhsT=w2_codes[:, m * P : (m + 1) * P].bitcast(FP8X4),
+                    lhsT_scale=w2_scales[:, m * P : (m + 1) * P],
+                    rhs=z_mx[a][0][:].bitcast(FP8X4),
+                    rhs_scale=z_mx[a][1][:],
+                    start=True,
+                    stop=True,
+                )
+                staged = sb(f"staged{a}_{m}", [P, HALF], F32)
+                if m == 1:
+                    nc.vector.tensor_copy(staged[:], res[:])
+                else:
+                    nc.scalar.copy(staged[:], res[:])
+                nc.sync.dma_start(out[m * P : (m + 1) * P, halves[a]], staged[:])

@@ -20,6 +20,7 @@ K_PASS = P * PACK
 PASSES = K // K_PASS
 HALF = S // 2
 LIST_ROWS = 16
+VECTOR_SHARE = 80
 
 
 def tile_picked_ycutmix_gelu_p_kernel(tc, x_words, x_scales, w1, w2, offs, give, take, out):
@@ -35,18 +36,15 @@ def tile_picked_ycutmix_gelu_p_kernel(tc, x_words, x_scales, w1, w2, offs, give,
         halves = [slice(0, HALF), slice(HALF, S)]
         whole = slice(0, S)
 
-        warm_in = sb("warm_in", [P, 8], F32)
-        warm_out = sb("warm_out", [P, 8], F32)
-        nc.vector.memset(warm_in[:], 0.0)
-        nc.scalar.activation(warm_out[:], warm_in[:], GELU)
-
         scale_rows = sb("scale_rows", [P, T], U8)
-        nc.gpsimd.memset(scale_rows[:].bitcast(I32), 0)
-        for q in range(4):
-            nc.gpsimd.dma_start(
-                scale_rows[32 * q : 32 * q + 4 * PASSES, :].bitcast(I32),
-                x_scales[:, 4 * q : 4 * q + 4, :].bitcast(I32),
-            )
+        nc.vector.memset(scale_rows[:].bitcast(I32), 0)
+
+        def load_scale_rows(o):
+            for q in range(4):
+                nc.sync.dma_start(
+                    scale_rows[32 * q + 4 * o : 32 * q + 4 * o + 4, :].bitcast(I32),
+                    x_scales[o, 4 * q : 4 * q + 4, :].bitcast(I32),
+                )
 
         w1_raw = [sb(f"w1_raw{o}", [P, PACK, H], F32) for o in range(PASSES)]
         x_tab = [sb(f"x_tab{o}", [P, T], U32) for o in range(PASSES)]
@@ -58,20 +56,22 @@ def tile_picked_ycutmix_gelu_p_kernel(tc, x_words, x_scales, w1, w2, offs, give,
         for o in range(PASSES):
             nc.sync.dma_start(w1_raw[o][:], w1[o * K_PASS : (o + 1) * K_PASS, :].rearrange("(p j) c -> p j c", j=PACK))
             if o == 0:
+                load_scale_rows(0)
                 nc.sync.dma_start(offs_sb[:], offs)
-        for o in range(PASSES):
             nc.sync.dma_start(x_tab[o][:].bitcast(I32), x_words[o].rearrange("p c r -> p (c r)").bitcast(I32))
+            if o == 0:
+                load_scale_rows(1)
         nc.sync.dma_start(w2_raw[:], w2.rearrange("(p j) n -> p j n", j=PACK))
         nc.sync.dma_start(give_sb[:], give)
         nc.sync.dma_start(take_sb[:], take)
 
-        w1_bf = [sb(f"w1_bf{o}", [P, H * PACK], BF16) for o in range(PASSES)]
-
-        def w1_views(o):
-            return (
-                w1_bf[o][:].rearrange("p (t m j) -> p m j t", t=PACK, j=PACK),
-                w1_raw[o][:].rearrange("p j (m t) -> p m j t", t=PACK),
-            )
+        def round_w1(o, tag=None):
+            values = sb(f"w1_bf{o}", [P, H * PACK], BF16, tag=tag)
+            dst = values[:].rearrange("p (t m j) -> p m j t", t=PACK, j=PACK)
+            src = w1_raw[o][:].rearrange("p j (m t) -> p m j t", t=PACK)
+            nc.vector.tensor_copy(dst[:, 0:VECTOR_SHARE], src[:, 0:VECTOR_SHARE])
+            nc.scalar.copy(dst[:, VECTOR_SHARE:P], src[:, VECTOR_SHARE:P])
+            return values
 
         def quantise(name, values, tag=None):
             width = values.shape[1] // PACK
@@ -90,28 +90,29 @@ def tile_picked_ycutmix_gelu_p_kernel(tc, x_words, x_scales, w1, w2, offs, give,
         pieces = [(0, halves[0]), (1, halves[0]), (0, halves[1]), (1, halves[1]), (2, whole), (3, whole)]
         acc = [psum.tile([P, cols.stop - cols.start], F32, name=f"acc{i}", tag=f"bank{i}") for i, (t, cols) in enumerate(pieces)]
 
-        def first_product(o, w_codes, w_scales, x_codes):
-            for i, (t, cols) in enumerate(pieces):
+        def first_product(o, which):
+            w_codes, w_scales = w1_mx[o]
+            for i in which:
+                t, cols = pieces[i]
                 nc.tensor.matmul_mx(
                     out=acc[i][:],
                     lhsT=w_codes[:, t * P : (t + 1) * P].bitcast(FP8X4),
                     lhsT_scale=w_scales[:, t * P : (t + 1) * P],
-                    rhs=x_codes[:, cols].bitcast(FP8X4),
+                    rhs=x_codes[o][:, cols].bitcast(FP8X4),
                     rhs_scale=x_scale[4 * o : P, cols],
                     start=(o == 0),
                     stop=(o == PASSES - 1),
                 )
 
-        nc.vector.tensor_copy(*w1_views(0))
-        nc.scalar.copy(*w1_views(1))
-        w1_mx0 = quantise("w1_0", w1_bf[0][:])
+        w1_mx = [quantise("w1_0", round_w1(0)[:])]
         x_scale = sb("x_scale", [P, S], U8)
         nc.vector.tensor_copy(x_scale[:], scale_rows[:].indirect(offs_sb[:]))
-        x_codes0 = pick_words(0, "scale_rows")
-        first_product(0, *w1_mx0, x_codes0)
-        w1_mx1 = quantise("w1_1", w1_bf[1][:], tag="x_tab0")
-        x_codes1 = pick_words(1, "w1_bf1")
-        first_product(1, *w1_mx1, x_codes1)
+        x_codes = [pick_words(0, None)]
+        w1_mx.append(quantise("w1_1", round_w1(1)[:], tag="scale_rows"))
+        x_codes.append(pick_words(1, "w1_bf1"))
+        for which in (range(0, 4), range(4, 6)):
+            for o in range(PASSES):
+                first_product(o, which)
 
         w2_bf = sb("w2_bf", [P, N * PACK], BF16, tag="x_tab1")
         nc.vector.tensor_copy(
@@ -120,7 +121,7 @@ def tile_picked_ycutmix_gelu_p_kernel(tc, x_words, x_scales, w1, w2, offs, give,
         )
 
         z = [sb(f"z{t}", [P, S], F32) for t in range(PACK)]
-        given = [sb(f"given{t}", [P, V], F32) for t in range(PACK)]
+        given = [sb(f"given{t}", [P, V], F32, tag="w2_raw" if t == 0 else None) for t in range(PACK)]
         for i, (t, cols) in enumerate(pieces):
             nc.scalar.activation(z[t][:, cols], acc[i][:], GELU)
 
@@ -147,14 +148,11 @@ def tile_picked_ycutmix_gelu_p_kernel(tc, x_words, x_scales, w1, w2, offs, give,
         w2_codes, w2_scales = quantise("w2", w2_bf[:], tag="given3")
 
         z_bf = [sb(f"z_bf{a}", [P, HALF * PACK], BF16) for a in range(2)]
-        nc.vector.tensor_copy(
-            z_bf[0][:].bitcast(I32).rearrange("p (c u) -> p c u", u=2),
-            pairs[0][:].bitcast(I32).rearrange("p (u c) -> p c u", u=2),
-        )
-        nc.scalar.copy(
-            z_bf[1][:].bitcast(U32).rearrange("p (c u) -> p c u", u=2),
-            pairs[1][:].bitcast(U32).rearrange("p (u c) -> p c u", u=2),
-        )
+        for a in range(2):
+            nc.vector.tensor_copy(
+                z_bf[a][:].bitcast(I32).rearrange("p (c u) -> p c u", u=2),
+                pairs[a][:].bitcast(I32).rearrange("p (u c) -> p c u", u=2),
+            )
         z_mx = [quantise(f"z{a}", z_bf[a][:]) for a in range(2)]
         for a in range(2):
             for m in range(N // P):

@@ -21,6 +21,8 @@ PASSES = K // K_PASS
 HALF = S // 2
 LIST_ROWS = 16
 VECTOR_SHARE = 80
+LATE = S - 32
+CHUNK = 128
 
 
 def tile_picked_ycutmix_gelu_p_kernel(tc, x_words, x_scales, w1, w2, offs, give, take, out):
@@ -110,65 +112,84 @@ def tile_picked_ycutmix_gelu_p_kernel(tc, x_words, x_scales, w1, w2, offs, give,
         x_codes = [pick_words(0, None)]
         w1_mx.append(quantise("w1_1", round_w1(1)[:], tag="scale_rows"))
         x_codes.append(pick_words(1, "w1_bf1"))
-        for which in (range(0, 4), range(4, 6)):
+        for which in (range(0, 4), (5, 4)):
             for o in range(PASSES):
                 first_product(o, which)
 
-        w2_bf = sb("w2_bf", [P, N * PACK], BF16, tag="x_tab1")
-        nc.vector.tensor_copy(
-            w2_bf[:].rearrange("p (c i j) -> p c j i", i=PACK, j=PACK),
-            w2_raw[:].rearrange("p j (c i) -> p c j i", i=PACK),
-        )
+        w2_bf = [sb(f"w2_bf{m}", [P, P * PACK], BF16) for m in range(N // P)]
+        for m in range(N // P):
+            nc.vector.tensor_copy(
+                w2_bf[m][:].rearrange("p (c i j) -> p c j i", i=PACK, j=PACK),
+                w2_raw[:, :, m * P : (m + 1) * P].rearrange("p j (c i) -> p c j i", i=PACK),
+            )
+        w2_mx = [quantise(f"w2_{m}", w2_bf[m][:]) for m in range(N // P)]
 
         z = [sb(f"z{t}", [P, S], F32) for t in range(PACK)]
-        given = [sb(f"given{t}", [P, V], F32, tag="w2_raw" if t == 0 else None) for t in range(PACK)]
-        for i, (t, cols) in enumerate(pieces):
+        first_given = sb("first_given", [P, 2, V], F32, tag="w2_bf0")
+        given = [first_given[:, 0, :], first_given[:, 1, :]] + [sb(f"given{t}", [P, V], F32)[:] for t in (2, 3)]
+        for i, (t, cols) in enumerate(pieces[:4]):
             nc.scalar.activation(z[t][:, cols], acc[i][:], GELU)
+        nc.scalar.activation(z[3][:, 0:LATE], acc[5][:, 0:LATE], GELU)
+        nc.scalar.activation(z[2][:], acc[4][:], GELU)
+        nc.scalar.activation(z[3][:, LATE:S], acc[5][:, LATE:S], GELU)
 
         def fetch(t):
-            nc.vector.tensor_copy(given[t][:], z[t][:].indirect(give_sb[:]))
+            nc.vector.tensor_copy(given[t], z[t][:].indirect(give_sb[:]))
 
         def put(t):
-            nc.vector.tensor_copy(z[t][:].indirect(take_sb[:]), given[t][:])
+            nc.vector.tensor_copy(z[t][:].indirect(take_sb[:]), given[t])
 
-        fetch(0)
-        for t in range(PACK):
-            if t + 1 < PACK:
-                fetch(t + 1)
+        for t in range(0, PACK, 2):
+            fetch(t)
+            fetch(t + 1)
             put(t)
+            put(t + 1)
 
-        pairs = [sb(f"pairs{a}", [P, HALF * PACK], BF16) for a in range(2)]
+        chunks = [slice(c * CHUNK, (c + 1) * CHUNK) for c in range(S // CHUNK)]
+        rounded = [sb(f"rounded{c}", [P, PACK, CHUNK], BF16) for c in range(len(chunks))]
         for t in range(PACK):
-            for a in range(2):
-                dst = pairs[a][:].rearrange("p (u c e) -> p u c e", u=2, e=2)[:, t // 2, :, t % 2]
-                if t >= 2 and a == 0:
-                    nc.vector.tensor_copy(dst, z[t][:, halves[a]])
-                else:
-                    nc.scalar.copy(dst, z[t][:, halves[a]])
-        w2_codes, w2_scales = quantise("w2", w2_bf[:], tag="given3")
+            for c in range(len(chunks)):
+                copy = nc.vector.tensor_copy if t == PACK - 1 and c < 2 else nc.scalar.copy
+                copy(rounded[c][:, t, :], z[t][:, chunks[c]])
 
-        z_bf = [sb(f"z_bf{a}", [P, HALF * PACK], BF16) for a in range(2)]
-        for a in range(2):
-            nc.vector.tensor_copy(
-                z_bf[a][:].bitcast(I32).rearrange("p (c u) -> p c u", u=2),
-                pairs[a][:].bitcast(I32).rearrange("p (u c) -> p c u", u=2),
+        out_rows = out.rearrange("(m p) c -> p m c", p=P)
+
+        def weave(c):
+            woven = sb(f"z_bf{c}", [P, CHUNK * PACK], BF16)
+            copy = nc.vector.tensor_copy if c < 2 else nc.scalar.copy
+            copy(
+                woven[:].rearrange("p (c i t) -> p c t i", i=PACK, t=PACK),
+                rounded[c][:].rearrange("p t (c i) -> p c t i", i=PACK),
             )
-        z_mx = [quantise(f"z{a}", z_bf[a][:]) for a in range(2)]
-        for a in range(2):
+            return woven
+
+        def second_product(c, z_codes, z_scales):
+            last = c == len(chunks) - 1
+            if last:
+                res = [psum.tile([P, CHUNK], F32, name=f"res{c}_{m}", tag=f"bank{c + m}")[:] for m in range(N // P)]
+            else:
+                bank = psum.tile([P, N // P, CHUNK], F32, name=f"res{c}", tag=f"bank{c}")
+                res = [bank[:, m, :] for m in range(N // P)]
             for m in range(N // P):
-                res = psum.tile([P, HALF], F32, name=f"res{a}_{m}", tag=f"bank{2 * a + m}")
                 nc.tensor.matmul_mx(
-                    out=res[:],
-                    lhsT=w2_codes[:, m * P : (m + 1) * P].bitcast(FP8X4),
-                    lhsT_scale=w2_scales[:, m * P : (m + 1) * P],
-                    rhs=z_mx[a][0][:].bitcast(FP8X4),
-                    rhs_scale=z_mx[a][1][:],
+                    out=res[m],
+                    lhsT=w2_mx[m][0][:].bitcast(FP8X4),
+                    lhsT_scale=w2_mx[m][1][:],
+                    rhs=z_codes[:].bitcast(FP8X4),
+                    rhs_scale=z_scales[:],
                     start=True,
                     stop=True,
                 )
-                staged = sb(f"staged{a}_{m}", [P, HALF], F32)
-                if m == 1:
-                    nc.vector.tensor_copy(staged[:], res[:])
-                else:
-                    nc.scalar.copy(staged[:], res[:])
-                nc.sync.dma_start(out[m * P : (m + 1) * P, halves[a]], staged[:])
+            staged = sb(f"staged{c}", [P, N // P, CHUNK], F32)
+            if last:
+                nc.vector.tensor_copy(staged[:, 0, :], res[0])
+                nc.scalar.copy(staged[:, 1, :], res[1])
+            else:
+                copy = nc.scalar.copy if c < 2 else nc.vector.tensor_copy
+                copy(staged[:], bank[:])
+            nc.sync.dma_start(out_rows[:, :, chunks[c]], staged[:])
+
+        woven = [weave(c) for c in range(len(chunks))]
+        z_mx = [quantise(f"z{c}", woven[c][:]) for c in range(len(chunks))]
+        for c in range(len(chunks)):
+            second_product(c, *z_mx[c])

@@ -20,8 +20,8 @@ K_PASS = P * PACK
 PASSES = K // K_PASS
 HALF = S // 2
 LIST_ROWS = 16
-VECTOR_SHARE = 80
-LATE = S - 32
+GROUPS = H // (PACK * PACK)
+VECTOR_SHARE = 20
 CHUNK = 128
 
 
@@ -63,16 +63,17 @@ def tile_picked_ycutmix_gelu_p_kernel(tc, x_words, x_scales, w1, w2, offs, give,
             nc.sync.dma_start(x_tab[o][:].bitcast(I32), x_words[o].rearrange("p c r -> p (c r)").bitcast(I32))
             if o == 0:
                 load_scale_rows(1)
-        nc.sync.dma_start(w2_raw[:], w2.rearrange("(p j) n -> p j n", j=PACK))
+        for t in range(PACK):
+            nc.sync.dma_start(w2_raw[:, t, :], w2.rearrange("(g t c) n -> t g c n", t=PACK, c=PACK)[t])
         nc.sync.dma_start(give_sb[:], give)
         nc.sync.dma_start(take_sb[:], take)
 
         def round_w1(o, tag=None):
             values = sb(f"w1_bf{o}", [P, H * PACK], BF16, tag=tag)
-            dst = values[:].rearrange("p (t m j) -> p m j t", t=PACK, j=PACK)
-            src = w1_raw[o][:].rearrange("p j (m t) -> p m j t", t=PACK)
-            nc.vector.tensor_copy(dst[:, 0:VECTOR_SHARE], src[:, 0:VECTOR_SHARE])
-            nc.scalar.copy(dst[:, VECTOR_SHARE:P], src[:, VECTOR_SHARE:P])
+            dst = values[:].rearrange("p (t g c j) -> p t g j c", t=PACK, c=PACK, j=PACK)
+            src = w1_raw[o][:].rearrange("p j (g t c) -> p t g j c", t=PACK, c=PACK)
+            nc.vector.tensor_copy(dst[:, :, 0:VECTOR_SHARE], src[:, :, 0:VECTOR_SHARE])
+            nc.scalar.copy(dst[:, :, VECTOR_SHARE:GROUPS], src[:, :, VECTOR_SHARE:GROUPS])
             return values
 
         def quantise(name, values, tag=None):
@@ -112,7 +113,7 @@ def tile_picked_ycutmix_gelu_p_kernel(tc, x_words, x_scales, w1, w2, offs, give,
         x_codes = [pick_words(0, None)]
         w1_mx.append(quantise("w1_1", round_w1(1)[:], tag="scale_rows"))
         x_codes.append(pick_words(1, "w1_bf1"))
-        for which in (range(0, 4), (5, 4)):
+        for which in (range(0, 4), range(4, 6)):
             for o in range(PASSES):
                 first_product(o, which)
 
@@ -125,13 +126,9 @@ def tile_picked_ycutmix_gelu_p_kernel(tc, x_words, x_scales, w1, w2, offs, give,
         w2_mx = [quantise(f"w2_{m}", w2_bf[m][:]) for m in range(N // P)]
 
         z = [sb(f"z{t}", [P, S], F32) for t in range(PACK)]
-        first_given = sb("first_given", [P, 2, V], F32, tag="w2_bf0")
-        given = [first_given[:, 0, :], first_given[:, 1, :]] + [sb(f"given{t}", [P, V], F32)[:] for t in (2, 3)]
-        for i, (t, cols) in enumerate(pieces[:4]):
+        given = [sb(f"given{t}", [P, V], F32, tag=f"w2_bf{t % 2}")[:] for t in range(PACK)]
+        for i, (t, cols) in enumerate(pieces):
             nc.scalar.activation(z[t][:, cols], acc[i][:], GELU)
-        nc.scalar.activation(z[3][:, 0:LATE], acc[5][:, 0:LATE], GELU)
-        nc.scalar.activation(z[2][:], acc[4][:], GELU)
-        nc.scalar.activation(z[3][:, LATE:S], acc[5][:, LATE:S], GELU)
 
         def fetch(t):
             nc.vector.tensor_copy(given[t], z[t][:].indirect(give_sb[:]))

@@ -23,6 +23,7 @@ LIST_ROWS = 16
 GROUPS = H // (PACK * PACK)
 VECTOR_SHARE = 20
 CHUNK = 128
+SPREAD = 4
 
 
 def tile_picked_ycutmix_gelu_p_kernel(tc, x_words, x_scales, w1, w2, offs, give, take, out):
@@ -40,40 +41,54 @@ def tile_picked_ycutmix_gelu_p_kernel(tc, x_words, x_scales, w1, w2, offs, give,
 
         scale_rows = sb("scale_rows", [P, T], U8)
         nc.vector.memset(scale_rows[:].bitcast(I32), 0)
-
-        def load_scale_rows(o):
-            for q in range(4):
-                nc.sync.dma_start(
-                    scale_rows[32 * q + 4 * o : 32 * q + 4 * o + 4, :].bitcast(I32),
-                    x_scales[o, 4 * q : 4 * q + 4, :].bitcast(I32),
-                )
+        x_scale = sb("x_scale", [P, PASSES, S], U8)
+        nc.vector.memset(x_scale[:].rearrange("p o c -> p (o c)").bitcast(I32), 0)
 
         w1_raw = [sb(f"w1_raw{o}", [P, PACK, H], F32) for o in range(PASSES)]
-        x_tab = [sb(f"x_tab{o}", [P, T], U32) for o in range(PASSES)]
-        w2_raw = sb("w2_raw", [P, PACK, N], F32)
         offs_sb = lists.tile([P, S // LIST_ROWS], U16, name="offs_sb")
         give_sb = lists.tile([P, V // LIST_ROWS], U16, name="give_sb")
         take_sb = lists.tile([P, V // LIST_ROWS], U16, name="take_sb")
 
-        for o in range(PASSES):
+        def load_w1(o):
             nc.sync.dma_start(w1_raw[o][:], w1[o * K_PASS : (o + 1) * K_PASS, :].rearrange("(p j) c -> p j c", j=PACK))
-            if o == 0:
-                load_scale_rows(0)
-                nc.sync.dma_start(offs_sb[:], offs)
-            nc.sync.dma_start(x_tab[o][:].bitcast(I32), x_words[o].rearrange("p c r -> p (c r)").bitcast(I32))
-            if o == 0:
-                load_scale_rows(1)
-        for t in range(PACK):
-            nc.sync.dma_start(w2_raw[:, t, :], w2.rearrange("(g t c) n -> t g c n", t=PACK, c=PACK)[t])
+
+        def load_words(o, tag=None):
+            table = sb(f"x_tab{o}", [P, T], U32, tag=tag)
+            nc.sync.dma_start(table[:].bitcast(I32), x_words[o].rearrange("p c r -> p (c r)").bitcast(I32))
+            return table
+
+        load_w1(0)
+        nc.sync.dma_start(scale_rows[0:P:SPREAD, :].bitcast(I32), x_scales.rearrange("o q c -> (o q) c").bitcast(I32))
+        nc.sync.dma_start(offs_sb[:], offs)
         nc.sync.dma_start(give_sb[:], give)
         nc.sync.dma_start(take_sb[:], take)
+        x_tab = [load_words(0)]
+        load_w1(1)
 
-        def round_w1(o, tag=None):
+        picked_rows = sb("picked_rows", [P, S], U8)
+        nc.vector.tensor_copy(picked_rows[:], scale_rows[:].indirect(offs_sb[:]))
+
+        def place_scale_rows(o, q):
+            first = SPREAD * (16 * o + 4 * q)
+            nc.sync.dma_start(
+                x_scale[32 * q + 4 * o : 32 * q + 4 * o + 4, o, :].bitcast(I32),
+                picked_rows[first : first + 4 * SPREAD : SPREAD, :].bitcast(I32),
+            )
+
+        places = [(o, q) for o in range(PASSES) for q in range(4)]
+        for o, q in places[:5]:
+            place_scale_rows(o, q)
+        x_tab.append(load_words(1, tag="scale_rows"))
+        for o, q in places[5:]:
+            place_scale_rows(o, q)
+
+        def round_w1(o, share, tag=None):
             values = sb(f"w1_bf{o}", [P, H * PACK], BF16, tag=tag)
             dst = values[:].rearrange("p (t g c j) -> p t g j c", t=PACK, c=PACK, j=PACK)
             src = w1_raw[o][:].rearrange("p j (g t c) -> p t g j c", t=PACK, c=PACK)
-            nc.vector.tensor_copy(dst[:, :, 0:VECTOR_SHARE], src[:, :, 0:VECTOR_SHARE])
-            nc.scalar.copy(dst[:, :, VECTOR_SHARE:GROUPS], src[:, :, VECTOR_SHARE:GROUPS])
+            if share:
+                nc.vector.tensor_copy(dst[:, :, 0:share], src[:, :, 0:share])
+            nc.scalar.copy(dst[:, :, share:GROUPS], src[:, :, share:GROUPS])
             return values
 
         def quantise(name, values, tag=None):
@@ -102,16 +117,17 @@ def tile_picked_ycutmix_gelu_p_kernel(tc, x_words, x_scales, w1, w2, offs, give,
                     lhsT=w_codes[:, t * P : (t + 1) * P].bitcast(FP8X4),
                     lhsT_scale=w_scales[:, t * P : (t + 1) * P],
                     rhs=x_codes[o][:, cols].bitcast(FP8X4),
-                    rhs_scale=x_scale[4 * o : P, cols],
+                    rhs_scale=x_scale[4 * o : P, o, cols],
                     start=(o == 0),
                     stop=(o == PASSES - 1),
                 )
 
-        w1_mx = [quantise("w1_0", round_w1(0)[:])]
-        x_scale = sb("x_scale", [P, S], U8)
-        nc.vector.tensor_copy(x_scale[:], scale_rows[:].indirect(offs_sb[:]))
+        w1_mx = [quantise("w1_0", round_w1(0, 0)[:])]
+        w2_raw = sb("w2_raw", [P, PACK, N], F32, tag="w1_raw0")
+        for t in range(PACK):
+            nc.sync.dma_start(w2_raw[:, t, :], w2.rearrange("(g t c) n -> t g c n", t=PACK, c=PACK)[t])
         x_codes = [pick_words(0, None)]
-        w1_mx.append(quantise("w1_1", round_w1(1)[:], tag="scale_rows"))
+        w1_mx.append(quantise("w1_1", round_w1(1, VECTOR_SHARE)[:], tag="w1_bf0"))
         x_codes.append(pick_words(1, "w1_bf1"))
         for which in (range(0, 4), range(4, 6)):
             for o in range(PASSES):

@@ -139,10 +139,10 @@ def tile_picked_ycutmix_gelu_p_kernel(tc, x_words, x_scales, w1, w2, offs, give,
                 w2_bf[m][:].rearrange("p (c i j) -> p c j i", i=PACK, j=PACK),
                 w2_raw[:, :, m * P : (m + 1) * P].rearrange("p j (c i) -> p c j i", i=PACK),
             )
-        w2_mx = [quantise(f"w2_{m}", w2_bf[m][:]) for m in range(N // P)]
+        w2_mx = [quantise("w2_0", w2_bf[0][:])]
 
         z = [sb(f"z{t}", [P, S], F32) for t in range(PACK)]
-        given = [sb(f"given{t}", [P, V], F32, tag=f"w2_bf{t % 2}")[:] for t in range(PACK)]
+        given = [sb(f"given{t}", [P, V], F32, tag=("w1_raw0", "w2_bf0")[t % 2])[:] for t in range(PACK)]
         for i, (t, cols) in enumerate(pieces):
             nc.scalar.activation(z[t][:, cols], acc[i][:], GELU)
 
@@ -158,6 +158,8 @@ def tile_picked_ycutmix_gelu_p_kernel(tc, x_words, x_scales, w1, w2, offs, give,
             put(t)
             put(t + 1)
 
+        w2_mx.append(quantise("w2_1", w2_bf[1][:], tag="w1_raw0"))
+
         chunks = [slice(c * CHUNK, (c + 1) * CHUNK) for c in range(S // CHUNK)]
         rounded = [sb(f"rounded{c}", [P, PACK, CHUNK], BF16) for c in range(len(chunks))]
         for t in range(PACK):
@@ -167,14 +169,13 @@ def tile_picked_ycutmix_gelu_p_kernel(tc, x_words, x_scales, w1, w2, offs, give,
 
         out_rows = out.rearrange("(m p) c -> p m c", p=P)
 
-        def weave(c):
-            woven = sb(f"z_bf{c}", [P, CHUNK * PACK], BF16)
-            copy = nc.vector.tensor_copy if c < 2 else nc.scalar.copy
+        woven = [sb(f"z_bf{c}", [P, CHUNK * PACK], BF16) for c in range(len(chunks))]
+
+        def weave(copy, c, groups):
             copy(
-                woven[:].rearrange("p (c i t) -> p c t i", i=PACK, t=PACK),
-                rounded[c][:].rearrange("p t (c i) -> p c t i", i=PACK),
+                woven[c][:].rearrange("p (c i t) -> p c t i", i=PACK, t=PACK)[:, groups],
+                rounded[c][:].rearrange("p t (c i) -> p c t i", i=PACK)[:, groups],
             )
-            return woven
 
         def second_product(c, z_codes, z_scales):
             last = c == len(chunks) - 1
@@ -202,7 +203,13 @@ def tile_picked_ycutmix_gelu_p_kernel(tc, x_words, x_scales, w1, w2, offs, give,
                 copy(staged[:], bank[:])
             nc.sync.dma_start(out_rows[:, :, chunks[c]], staged[:])
 
-        woven = [weave(c) for c in range(len(chunks))]
-        z_mx = [quantise(f"z{c}", woven[c][:]) for c in range(len(chunks))]
+        groups = CHUNK // PACK
+        weave(nc.vector.tensor_copy, 0, slice(0, groups))
+        weave(nc.vector.tensor_copy, 1, slice(0, groups))
+        weave(nc.scalar.copy, 2, slice(0, groups))
+        weave(nc.scalar.copy, 3, slice(0, groups // 2))
+        z_mx = [quantise("z0", woven[0][:])]
+        weave(nc.vector.tensor_copy, 3, slice(groups // 2, groups))
+        z_mx.extend(quantise(f"z{c}", woven[c][:]) for c in range(1, len(chunks)))
         for c in range(len(chunks)):
             second_product(c, *z_mx[c])

@@ -201,7 +201,8 @@ def tile_picked_ycutmix_gelu_p_kernel(tc, x_words, x_scales, w1, w2, offs, give,
             else:
                 copy = nc.scalar.copy if c < 2 else nc.vector.tensor_copy
                 copy(staged[:], bank[:])
-            nc.sync.dma_start(out_rows[:, :, chunks[c]], staged[:])
+            queue = nc.scalar if c % 2 else nc.sync
+            queue.dma_start(out_rows[:, :, chunks[c]], staged[:])
 
         groups = CHUNK // PACK
         weave(nc.vector.tensor_copy, 0, slice(0, groups))

@@ -34,7 +34,7 @@ def tile_picked_ycutmix_gelu_p_kernel(tc, x_words, x_scales, w1, w2, offs, give,
         psum = ctx.enter_context(tc.psum_pool(name="psum", bufs=1))
 
         def sb(name, shape, dtype, tag=None):
-            return keep.tile(shape, dtype, name=name, tag=tag or name, align_bytes=64)
+            return keep.tile(shape, dtype, name=name, tag=tag or name, align_bytes=256)
 
         halves = [slice(0, HALF), slice(HALF, S)]
         whole = slice(0, S)

@@ -13,6 +13,9 @@ U16 = mybir.dt.uint16
 U8 = mybir.dt.uint8
 FP8X4 = mybir.dt.float8_e4m3fn_x4
 GELU = mybir.ActivationFunctionType.Gelu_apprx_tanh
+COPY = mybir.ActivationFunctionType.Copy
+MULT = mybir.AluOpType.mult
+ADD = mybir.AluOpType.add
 
 P = 128
 PACK = 4
@@ -133,39 +136,35 @@ def tile_picked_ycutmix_gelu_p_kernel(tc, x_words, x_scales, w1, w2, offs, give,
             for o in range(PASSES):
                 first_product(o, which)
 
-        w2_bf = [sb(f"w2_bf{m}", [P, P * PACK], BF16) for m in range(N // P)]
-        for m in range(N // P):
-            nc.vector.tensor_copy(
-                w2_bf[m][:].rearrange("p (c i j) -> p c j i", i=PACK, j=PACK),
-                w2_raw[:, :, m * P : (m + 1) * P].rearrange("p j (c i) -> p c j i", i=PACK),
-            )
-        w2_mx = [quantise("w2_0", w2_bf[0][:])]
+        w2_bf = sb("w2_bf", [P, N, PACK], BF16)
+        nc.gpsimd.tensor_scalar(w2_bf[:], w2_raw[:].rearrange("p j c -> p c j"), 1.0, 0.0, MULT, ADD)
 
         z = [sb(f"z{t}", [P, S], F32) for t in range(PACK)]
-        given = [sb(f"given{t}", [P, V], F32, tag=("w1_raw0", "w2_bf0")[t % 2])[:] for t in range(PACK)]
+        given = [sb(f"given{t}", [P, V], F32)[:] for t in range(PACK)]
         for i, (t, cols) in enumerate(pieces):
             nc.scalar.activation(z[t][:, cols], acc[i][:], GELU)
 
-        def fetch(t):
+        for t in (0, 1):
             nc.vector.tensor_copy(given[t], z[t][:].indirect(give_sb[:]))
-
-        def put(t):
+        for t in (2, 3):
+            nc.scalar.activation(given[t], z[t][:].indirect(give_sb[:]), COPY)
+        for t in (0, 1):
             nc.vector.tensor_copy(z[t][:].indirect(take_sb[:]), given[t])
+        nc.scalar.activation(z[2][:].indirect(take_sb[:]), given[2], COPY)
+        nc.vector.tensor_copy(z[3][:].indirect(take_sb[:]), given[3])
 
-        for t in range(0, PACK, 2):
-            fetch(t)
-            fetch(t + 1)
-            put(t)
-            put(t + 1)
-
-        w2_mx.append(quantise("w2_1", w2_bf[1][:], tag="w1_raw0"))
+        w2_codes, w2_scales = quantise("w2", w2_bf[:].rearrange("p c j -> p (c j)"), tag="given3")
 
         chunks = [slice(c * CHUNK, (c + 1) * CHUNK) for c in range(S // CHUNK)]
-        rounded = [sb(f"rounded{c}", [P, PACK, CHUNK], BF16) for c in range(len(chunks))]
-        for t in range(PACK):
-            for c in range(len(chunks)):
-                copy = nc.vector.tensor_copy if t == PACK - 1 and c < 2 else nc.scalar.copy
-                copy(rounded[c][:, t, :], z[t][:, chunks[c]])
+        rounded_all = sb("rounded", [P, 2, PACK, HALF], BF16, tag="w1_raw0")
+        rounded = [rounded_all[:, a] for a in range(2)]
+        for t in (0, 1):
+            for a in range(2):
+                nc.gpsimd.tensor_scalar(rounded[a][:, t, :], z[t][:, halves[a]], 1.0, 0.0, MULT, ADD)
+        for a in range(2):
+            nc.scalar.copy(rounded[a][:, 2, :], z[2][:, halves[a]])
+        nc.vector.tensor_copy(rounded[0][:, 3, :], z[3][:, halves[0]])
+        nc.scalar.copy(rounded[1][:, 3, :], z[3][:, halves[1]])
 
         out_rows = out.rearrange("(m p) c -> p m c", p=P)
 
@@ -174,7 +173,7 @@ def tile_picked_ycutmix_gelu_p_kernel(tc, x_words, x_scales, w1, w2, offs, give,
         def weave(copy, c, groups):
             copy(
                 woven[c][:].rearrange("p (c i t) -> p c t i", i=PACK, t=PACK)[:, groups],
-                rounded[c][:].rearrange("p t (c i) -> p c t i", i=PACK)[:, groups],
+                rounded[c // 2][:, :, chunks[c % 2]].rearrange("p t (c i) -> p c t i", i=PACK)[:, groups],
             )
 
         def second_product(c, z_codes, z_scales):
@@ -187,8 +186,8 @@ def tile_picked_ycutmix_gelu_p_kernel(tc, x_words, x_scales, w1, w2, offs, give,
             for m in range(N // P):
                 nc.tensor.matmul_mx(
                     out=res[m],
-                    lhsT=w2_mx[m][0][:].bitcast(FP8X4),
-                    lhsT_scale=w2_mx[m][1][:],
+                    lhsT=w2_codes[:, m * P : (m + 1) * P].bitcast(FP8X4),
+                    lhsT_scale=w2_scales[:, m * P : (m + 1) * P],
                     rhs=z_codes[:].bitcast(FP8X4),
                     rhs_scale=z_scales[:],
                     start=True,

@@ -14,8 +14,6 @@ U8 = mybir.dt.uint8
 FP8X4 = mybir.dt.float8_e4m3fn_x4
 GELU = mybir.ActivationFunctionType.Gelu_apprx_tanh
 COPY = mybir.ActivationFunctionType.Copy
-MULT = mybir.AluOpType.mult
-ADD = mybir.AluOpType.add
 
 P = 128
 PACK = 4
@@ -34,6 +32,7 @@ def tile_picked_ycutmix_gelu_p_kernel(tc, x_words, x_scales, w1, w2, offs, give,
     with ExitStack() as ctx:
         lists = ctx.enter_context(tc.tile_pool(name="lists", bufs=1))
         keep = ctx.enter_context(tc.tile_pool(name="keep", bufs=1))
+        shared = ctx.enter_context(tc.tile_pool(name="shared", bufs=1))
         psum = ctx.enter_context(tc.psum_pool(name="psum", bufs=1))
 
         def sb(name, shape, dtype, tag=None):
@@ -136,11 +135,20 @@ def tile_picked_ycutmix_gelu_p_kernel(tc, x_words, x_scales, w1, w2, offs, give,
             for o in range(PASSES):
                 first_product(o, which)
 
-        w2_bf = sb("w2_bf", [P, N, PACK], BF16)
-        nc.gpsimd.tensor_scalar(w2_bf[:], w2_raw[:].rearrange("p j c -> p c j"), 1.0, 0.0, MULT, ADD)
+        w2_bf = shared.tile([P, N * PACK], BF16, name="w2_bf", offset=0, align_bytes=256)
+        w2_codes = sb("w2_codes", [P, N], U32)
+        w2_scales = sb("w2_scales", [P, N], U8)
+        blocks = [slice(m * P, (m + 1) * P) for m in range(N // P)]
+        for m in range(N // P):
+            nc.vector.tensor_copy(
+                w2_bf[:, m * P * PACK : (m + 1) * P * PACK].rearrange("p (c i j) -> p c j i", i=PACK, j=PACK),
+                w2_raw[:, :, blocks[m]].rearrange("p j (c i) -> p c j i", i=PACK),
+            )
+        for m in range(N // P):
+            nc.vector.quantize_mx(out=w2_codes[:, blocks[m]].bitcast(FP8X4), scales=w2_scales[:, blocks[m]], in_=w2_bf[:, m * P * PACK : (m + 1) * P * PACK])
 
         z = [sb(f"z{t}", [P, S], F32) for t in range(PACK)]
-        given = [sb(f"given{t}", [P, V], F32)[:] for t in range(PACK)]
+        given = [shared.tile([P, V], F32, name=f"given{t}", offset=t * V * 4, align_bytes=256)[:] for t in range(PACK)]
         for i, (t, cols) in enumerate(pieces):
             nc.scalar.activation(z[t][:, cols], acc[i][:], GELU)
 
@@ -150,21 +158,18 @@ def tile_picked_ycutmix_gelu_p_kernel(tc, x_words, x_scales, w1, w2, offs, give,
             nc.scalar.activation(given[t], z[t][:].indirect(give_sb[:]), COPY)
         for t in (0, 1):
             nc.vector.tensor_copy(z[t][:].indirect(take_sb[:]), given[t])
-        nc.scalar.activation(z[2][:].indirect(take_sb[:]), given[2], COPY)
-        nc.vector.tensor_copy(z[3][:].indirect(take_sb[:]), given[3])
-
-        w2_codes, w2_scales = quantise("w2", w2_bf[:].rearrange("p c j -> p (c j)"), tag="given3")
+        cut = V // LIST_ROWS // 2
+        nc.scalar.activation(z[2][:].indirect(take_sb[:, 0:cut]), given[2][:, 0 : V // 2], COPY)
+        nc.vector.tensor_copy(z[2][:].indirect(take_sb[:, cut : 2 * cut]), given[2][:, V // 2 : V])
+        nc.scalar.activation(z[3][:].indirect(take_sb[:]), given[3], COPY)
 
         chunks = [slice(c * CHUNK, (c + 1) * CHUNK) for c in range(S // CHUNK)]
-        rounded_all = sb("rounded", [P, 2, PACK, HALF], BF16, tag="w1_raw0")
-        rounded = [rounded_all[:, a] for a in range(2)]
+        rounded = sb("rounded", [P, PACK, S], BF16)
         for t in (0, 1):
-            for a in range(2):
-                nc.gpsimd.tensor_scalar(rounded[a][:, t, :], z[t][:, halves[a]], 1.0, 0.0, MULT, ADD)
+            nc.vector.tensor_copy(rounded[:, t, :], z[t][:])
         for a in range(2):
-            nc.scalar.copy(rounded[a][:, 2, :], z[2][:, halves[a]])
-        nc.vector.tensor_copy(rounded[0][:, 3, :], z[3][:, halves[0]])
-        nc.scalar.copy(rounded[1][:, 3, :], z[3][:, halves[1]])
+            nc.vector.tensor_copy(rounded[:, 3, halves[a]], z[3][:, halves[a]])
+            nc.scalar.copy(rounded[:, 2, halves[a]], z[2][:, halves[a]])
 
         out_rows = out.rearrange("(m p) c -> p m c", p=P)
 
@@ -173,7 +178,7 @@ def tile_picked_ycutmix_gelu_p_kernel(tc, x_words, x_scales, w1, w2, offs, give,
         def weave(copy, c, groups):
             copy(
                 woven[c][:].rearrange("p (c i t) -> p c t i", i=PACK, t=PACK)[:, groups],
-                rounded[c // 2][:, :, chunks[c % 2]].rearrange("p t (c i) -> p c t i", i=PACK)[:, groups],
+                rounded[:, :, chunks[c]].rearrange("p t (c i) -> p c t i", i=PACK)[:, groups],
             )
 
         def second_product(c, z_codes, z_scales):

@@ -39,7 +39,6 @@ def tile_picked_ycutmix_gelu_p_kernel(tc, x_words, x_scales, w1, w2, offs, give,
             return keep.tile(shape, dtype, name=name, tag=tag or name, align_bytes=256)
 
         halves = [slice(0, HALF), slice(HALF, S)]
-        whole = slice(0, S)
 
         scale_rows = sb("scale_rows", [P, T], U8)
         nc.vector.memset(scale_rows[:].bitcast(I32), 0)
@@ -100,40 +99,51 @@ def tile_picked_ycutmix_gelu_p_kernel(tc, x_words, x_scales, w1, w2, offs, give,
             nc.vector.quantize_mx(out=codes[:].bitcast(FP8X4), scales=scales[:], in_=values)
             return codes, scales
 
-        def pick_words(o, tag):
+        def pick_words(o, tag, runs):
             picked = sb(f"x_codes{o}", [P, S], U32, tag=tag)
-            half_cols = HALF // LIST_ROWS
-            for a in range(2):
-                nc.vector.tensor_copy(picked[:, halves[a]], x_tab[o][:].indirect(offs_sb[:, a * half_cols : (a + 1) * half_cols]))
+            for cols in runs:
+                nc.vector.tensor_copy(picked[:, cols], x_tab[o][:].indirect(offs_sb[:, cols.start // LIST_ROWS : cols.stop // LIST_ROWS]))
             return picked
 
-        pieces = [(0, halves[0]), (1, halves[0]), (0, halves[1]), (1, halves[1]), (2, whole), (3, whole)]
-        acc = [psum.tile([P, cols.stop - cols.start], F32, name=f"acc{i}", tag=f"bank{i}") for i, (t, cols) in enumerate(pieces)]
+        first, middle, last = slice(0, 128), slice(128, 384), slice(384, 512)
+        banks = [
+            [(0, first)],
+            [(1, first)],
+            [(2, first), (3, first)],
+            [(0, middle)],
+            [(0, last)],
+            [(1, middle), (1, last)],
+            [(2, middle), (2, last)],
+            [(3, middle), (3, last)],
+        ]
+        acc = [psum.tile([P, sum(c.stop - c.start for t, c in b)], F32, name=f"acc{i}", tag=f"bank{i}") for i, b in enumerate(banks)]
 
-        def first_product(o, which):
+        def first_product(o):
             w_codes, w_scales = w1_mx[o]
-            for i in which:
-                t, cols = pieces[i]
-                nc.tensor.matmul_mx(
-                    out=acc[i][:],
-                    lhsT=w_codes[:, t * P : (t + 1) * P].bitcast(FP8X4),
-                    lhsT_scale=w_scales[:, t * P : (t + 1) * P],
-                    rhs=x_codes[o][:, cols].bitcast(FP8X4),
-                    rhs_scale=x_scale[4 * o : P, o, cols],
-                    start=(o == 0),
-                    stop=(o == PASSES - 1),
-                )
+            for i, bank in enumerate(banks):
+                at = 0
+                for n, (t, cols) in enumerate(bank):
+                    width = cols.stop - cols.start
+                    nc.tensor.matmul_mx(
+                        out=acc[i][:, at : at + width],
+                        lhsT=w_codes[:, t * P : (t + 1) * P].bitcast(FP8X4),
+                        lhsT_scale=w_scales[:, t * P : (t + 1) * P],
+                        rhs=x_codes[o][:, cols].bitcast(FP8X4),
+                        rhs_scale=x_scale[4 * o : P, o, cols],
+                        start=(o == 0 and n == 0),
+                        stop=(o == PASSES - 1 and n == len(bank) - 1),
+                    )
+                    at = at + width
 
         w1_mx = [quantise("w1_0", round_w1(0, 0)[:])]
         w2_raw = sb("w2_raw", [P, PACK, N], F32, tag="w1_raw0")
         for t in range(PACK):
             nc.sync.dma_start(w2_raw[:, t, :], w2.rearrange("(g t c) n -> t g c n", t=PACK, c=PACK)[t])
-        x_codes = [pick_words(0, None)]
+        x_codes = [pick_words(0, None, halves)]
         w1_mx.append(quantise("w1_1", round_w1(1, VECTOR_SHARE)[:], tag="w1_bf0"))
-        x_codes.append(pick_words(1, "w1_bf1"))
-        for which in (range(0, 4), range(4, 6)):
-            for o in range(PASSES):
-                first_product(o, which)
+        x_codes.append(pick_words(1, "w1_bf1", (first, middle, last)))
+        for o in range(PASSES):
+            first_product(o)
 
         w2_bf = shared.tile([P, N * PACK], BF16, name="w2_bf", offset=0, align_bytes=256)
         w2_codes = sb("w2_codes", [P, N], U32)
@@ -149,8 +159,12 @@ def tile_picked_ycutmix_gelu_p_kernel(tc, x_words, x_scales, w1, w2, offs, give,
 
         z = [sb(f"z{t}", [P, S], F32) for t in range(PACK)]
         given = [shared.tile([P, V], F32, name=f"given{t}", offset=t * V * 4, align_bytes=256)[:] for t in range(PACK)]
-        for i, (t, cols) in enumerate(pieces):
-            nc.scalar.activation(z[t][:, cols], acc[i][:], GELU)
+        for i, bank in enumerate(banks):
+            if bank[0][0] == bank[-1][0]:
+                nc.scalar.activation(z[bank[0][0]][:, bank[0][1].start : bank[-1][1].stop], acc[i][:], GELU)
+            else:
+                for n, (t, cols) in enumerate(bank):
+                    nc.scalar.activation(z[t][:, cols], acc[i][:, n * P : (n + 1) * P], GELU)
 
         for t in (0, 1):
             nc.vector.tensor_copy(given[t], z[t][:].indirect(give_sb[:]))

@@ -172,18 +172,17 @@ def tile_picked_ycutmix_gelu_p_kernel(tc, x_words, x_scales, w1, w2, offs, give,
             nc.scalar.activation(given[t], z[t][:].indirect(give_sb[:]), COPY)
         for t in (0, 1):
             nc.vector.tensor_copy(z[t][:].indirect(take_sb[:]), given[t])
-        cut = V // LIST_ROWS // 2
-        nc.scalar.activation(z[2][:].indirect(take_sb[:, 0:cut]), given[2][:, 0 : V // 2], COPY)
-        nc.vector.tensor_copy(z[2][:].indirect(take_sb[:, cut : 2 * cut]), given[2][:, V // 2 : V])
-        nc.scalar.activation(z[3][:].indirect(take_sb[:]), given[3], COPY)
+        for t in (2, 3):
+            nc.scalar.activation(z[t][:].indirect(take_sb[:]), given[t], COPY)
 
         chunks = [slice(c * CHUNK, (c + 1) * CHUNK) for c in range(S // CHUNK)]
         rounded = sb("rounded", [P, PACK, S], BF16)
         for t in (0, 1):
             nc.vector.tensor_copy(rounded[:, t, :], z[t][:])
+        nc.vector.tensor_copy(rounded[:, 2, halves[0]], z[2][:, halves[0]])
+        nc.scalar.copy(rounded[:, 2, halves[1]], z[2][:, halves[1]])
         for a in range(2):
             nc.vector.tensor_copy(rounded[:, 3, halves[a]], z[3][:, halves[a]])
-            nc.scalar.copy(rounded[:, 2, halves[a]], z[2][:, halves[a]])
 
         out_rows = out.rearrange("(m p) c -> p m c", p=P)
 
@@ -223,12 +222,8 @@ def tile_picked_ycutmix_gelu_p_kernel(tc, x_words, x_scales, w1, w2, offs, give,
             queue.dma_start(out_rows[:, :, chunks[c]], staged[:])
 
         groups = CHUNK // PACK
-        weave(nc.vector.tensor_copy, 0, slice(0, groups))
-        weave(nc.vector.tensor_copy, 1, slice(0, groups))
-        weave(nc.scalar.copy, 2, slice(0, groups))
-        weave(nc.scalar.copy, 3, slice(0, groups // 2))
-        z_mx = [quantise("z0", woven[0][:])]
-        weave(nc.vector.tensor_copy, 3, slice(groups // 2, groups))
-        z_mx.extend(quantise(f"z{c}", woven[c][:]) for c in range(1, len(chunks)))
+        for c in range(len(chunks)):
+            weave(nc.scalar.copy if c % 2 else nc.vector.tensor_copy, c, slice(0, groups))
+        z_mx = [quantise(f"z{c}", woven[c][:]) for c in range(len(chunks))]
         for c in range(len(chunks)):
             second_product(c, *z_mx[c])

@@ -22,7 +22,7 @@ PASSES = K // K_PASS
 HALF = S // 2
 LIST_ROWS = 16
 GROUPS = H // (PACK * PACK)
-VECTOR_SHARE = 20
+VECTOR_SHARE = 16
 CHUNK = 128
 SPREAD = 4
 
@@ -83,14 +83,11 @@ def tile_picked_ycutmix_gelu_p_kernel(tc, x_words, x_scales, w1, w2, offs, give,
         for o, q in places[5:]:
             place_scale_rows(o, q)
 
-        def round_w1(o, share, tag=None):
-            values = sb(f"w1_bf{o}", [P, H * PACK], BF16, tag=tag)
-            dst = values[:].rearrange("p (t g c j) -> p t g j c", t=PACK, c=PACK, j=PACK)
+        def round_w1(copy, o, values, planes, groups):
+            dst = values[:].rearrange("p (t g c j) -> p t g j c", g=GROUPS, c=PACK, j=PACK)
             src = w1_raw[o][:].rearrange("p j (g t c) -> p t g j c", t=PACK, c=PACK)
-            if share:
-                nc.vector.tensor_copy(dst[:, :, 0:share], src[:, :, 0:share])
-            nc.scalar.copy(dst[:, :, share:GROUPS], src[:, :, share:GROUPS])
-            return values
+            first = planes.start % dst.shape[1]
+            copy(dst[:, first : first + planes.stop - planes.start, groups], src[:, planes, groups])
 
         def quantise(name, values, tag=None):
             width = values.shape[1] // PACK
@@ -119,15 +116,15 @@ def tile_picked_ycutmix_gelu_p_kernel(tc, x_words, x_scales, w1, w2, offs, give,
         acc = [psum.tile([P, sum(c.stop - c.start for t, c in b)], F32, name=f"acc{i}", tag=f"bank{i}") for i, b in enumerate(banks)]
 
         def first_product(o):
-            w_codes, w_scales = w1_mx[o]
             for i, bank in enumerate(banks):
                 at = 0
                 for n, (t, cols) in enumerate(bank):
                     width = cols.stop - cols.start
+                    w_codes, w_scales = w1_mx[o][t]
                     nc.tensor.matmul_mx(
                         out=acc[i][:, at : at + width],
-                        lhsT=w_codes[:, t * P : (t + 1) * P].bitcast(FP8X4),
-                        lhsT_scale=w_scales[:, t * P : (t + 1) * P],
+                        lhsT=w_codes.bitcast(FP8X4),
+                        lhsT_scale=w_scales,
                         rhs=x_codes[o][:, cols].bitcast(FP8X4),
                         rhs_scale=x_scale[4 * o : P, o, cols],
                         start=(o == 0 and n == 0),
@@ -135,13 +132,25 @@ def tile_picked_ycutmix_gelu_p_kernel(tc, x_words, x_scales, w1, w2, offs, give,
                     )
                     at = at + width
 
-        w1_mx = [quantise("w1_0", round_w1(0, 0)[:])]
+        def by_plane(codes, scales):
+            return [(codes[:, t * P : (t + 1) * P], scales[:, t * P : (t + 1) * P]) for t in range(codes.shape[1] // P)]
+
+        every = slice(0, GROUPS)
+        w1_bf = sb("w1_bf0", [P, H * PACK], BF16)
+        round_w1(nc.scalar.copy, 0, w1_bf, slice(0, PACK), every)
+        w1_mx = [by_plane(*quantise("w1_0", w1_bf[:]))]
         w2_raw = sb("w2_raw", [P, PACK, N], F32, tag="w1_raw0")
         for t in range(PACK):
             nc.sync.dma_start(w2_raw[:, t, :], w2.rearrange("(g t c) n -> t g c n", t=PACK, c=PACK)[t])
         x_codes = [pick_words(0, None, halves)]
-        w1_mx.append(quantise("w1_1", round_w1(1, VECTOR_SHARE)[:], tag="w1_bf0"))
-        x_codes.append(pick_words(1, "w1_bf1", (first, middle, last)))
+        low = sb("w1_low", [P, H * PACK // 2], BF16)
+        high = sb("w1_high", [P, H * PACK // 2], BF16)
+        round_w1(nc.vector.tensor_copy, 1, low, slice(0, 2), every)
+        round_w1(nc.vector.tensor_copy, 1, high, slice(2, 3), slice(0, VECTOR_SHARE))
+        round_w1(nc.scalar.copy, 1, high, slice(3, 4), every)
+        round_w1(nc.scalar.copy, 1, high, slice(2, 3), slice(VECTOR_SHARE, GROUPS))
+        w1_mx.append(by_plane(*quantise("w1_low", low[:])) + by_plane(*quantise("w1_high", high[:])))
+        x_codes.append(pick_words(1, None, (first, middle, last)))
         for o in range(PASSES):
             first_product(o)
 

@@ -167,7 +167,10 @@ def tile_picked_ycutmix_gelu_p_kernel(tc, x_words, x_scales, w1, w2, offs, give,
             nc.vector.quantize_mx(out=w2_codes[:, blocks[m]].bitcast(FP8X4), scales=w2_scales[:, blocks[m]], in_=w2_bf[:, m * P * PACK : (m + 1) * P * PACK])
 
         z = [sb(f"z{t}", [P, S], F32) for t in range(PACK)]
-        given = [shared.tile([P, V], F32, name=f"given{t}", offset=t * V * 4, align_bytes=256)[:] for t in range(PACK)]
+        given = {t: shared.tile([P, V], F32, name=f"given{t}", offset=i * V * 4, align_bytes=256)[:] for i, t in enumerate((0, 1, 3))}
+        given_late = shared.tile([P, V // 2], F32, name="given_late", offset=3 * V * 4, align_bytes=256)
+        given_early = shared.tile([P, V // 2], F32, name="given_early", offset=7 * V * 2, align_bytes=256)
+        early, late = slice(0, V // LIST_ROWS // 2), slice(V // LIST_ROWS // 2, V // LIST_ROWS)
         for i, bank in enumerate(banks):
             if bank[0][0] == bank[-1][0]:
                 nc.scalar.activation(z[bank[0][0]][:, bank[0][1].start : bank[-1][1].stop], acc[i][:], GELU)
@@ -177,21 +180,22 @@ def tile_picked_ycutmix_gelu_p_kernel(tc, x_words, x_scales, w1, w2, offs, give,
 
         for t in (0, 1):
             nc.vector.tensor_copy(given[t], z[t][:].indirect(give_sb[:]))
-        for t in (2, 3):
-            nc.scalar.activation(given[t], z[t][:].indirect(give_sb[:]), COPY)
+        nc.scalar.activation(given_early[:], z[2][:].indirect(give_sb[:, early]), COPY)
+        nc.scalar.activation(given_late[:], z[2][:].indirect(give_sb[:, late]), COPY)
+        nc.scalar.activation(given[3], z[3][:].indirect(give_sb[:]), COPY)
         for t in (0, 1):
             nc.vector.tensor_copy(z[t][:].indirect(take_sb[:]), given[t])
-        for t in (2, 3):
-            nc.scalar.activation(z[t][:].indirect(take_sb[:]), given[t], COPY)
+        nc.scalar.activation(z[2][:].indirect(take_sb[:, early]), given_early[:], COPY)
+        nc.scalar.activation(z[3][:].indirect(take_sb[:]), given[3], COPY)
+        nc.vector.tensor_copy(z[2][:].indirect(take_sb[:, late]), given_late[:])
 
         chunks = [slice(c * CHUNK, (c + 1) * CHUNK) for c in range(S // CHUNK)]
-        rounded = sb("rounded", [P, PACK, S], BF16)
-        for t in (0, 1):
-            nc.vector.tensor_copy(rounded[:, t, :], z[t][:])
-        nc.vector.tensor_copy(rounded[:, 2, halves[0]], z[2][:, halves[0]])
-        nc.scalar.copy(rounded[:, 2, halves[1]], z[2][:, halves[1]])
+        rounded = shared.tile([P, PACK, S], BF16, name="rounded", offset=7 * V * 2, align_bytes=256)
+        nc.scalar.copy(rounded[:, 0, :], z[0][:])
+        nc.vector.tensor_copy(rounded[:, 1, :], z[1][:])
         for a in range(2):
-            nc.vector.tensor_copy(rounded[:, 3, halves[a]], z[3][:, halves[a]])
+            for t in (2, 3):
+                nc.vector.tensor_copy(rounded[:, t, halves[a]], z[t][:, halves[a]])
 
         out_rows = out.rearrange("(m p) c -> p m c", p=P)
 

@@ -14,6 +14,7 @@ U8 = mybir.dt.uint8
 FP8X4 = mybir.dt.float8_e4m3fn_x4
 GELU = mybir.ActivationFunctionType.Gelu_apprx_tanh
 COPY = mybir.ActivationFunctionType.Copy
+MULT = mybir.AluOpType.mult
 
 P = 128
 PACK = 4
@@ -166,7 +167,10 @@ def tile_picked_ycutmix_gelu_p_kernel(tc, x_words, x_scales, w1, w2, offs, give,
         for m in range(N // P):
             nc.vector.quantize_mx(out=w2_codes[:, blocks[m]].bitcast(FP8X4), scales=w2_scales[:, blocks[m]], in_=w2_bf[:, m * P * PACK : (m + 1) * P * PACK])
 
-        z = [sb(f"z{t}", [P, S], F32) for t in range(PACK)]
+        planes = shared.tile([P, PACK * S], F32, name="planes", offset=N * PACK * 2, align_bytes=256)
+        ones = shared.tile([P, V], F32, name="ones", offset=N * PACK * 2 + PACK * S * 4, align_bytes=256)
+        nc.gpsimd.memset(ones[:], 1.0)
+        z = [planes[:, 0:S]] + [sb(f"z{t}", [P, S], F32)[:] for t in range(1, PACK)]
         given = {t: shared.tile([P, V], F32, name=f"given{t}", offset=i * V * 4, align_bytes=256)[:] for i, t in enumerate((0, 1, 3))}
         given_late = shared.tile([P, V // 2], F32, name="given_late", offset=3 * V * 4, align_bytes=256)
         given_early = shared.tile([P, V // 2], F32, name="given_early", offset=7 * V * 2, align_bytes=256)
@@ -183,19 +187,19 @@ def tile_picked_ycutmix_gelu_p_kernel(tc, x_words, x_scales, w1, w2, offs, give,
         nc.scalar.activation(given_early[:], z[2][:].indirect(give_sb[:, early]), COPY)
         nc.scalar.activation(given_late[:], z[2][:].indirect(give_sb[:, late]), COPY)
         nc.scalar.activation(given[3], z[3][:].indirect(give_sb[:]), COPY)
-        for t in (0, 1):
-            nc.vector.tensor_copy(z[t][:].indirect(take_sb[:]), given[t])
+        nc.vector.tensor_tensor(planes[:].indirect(take_sb[:]), given[0], ones[:], MULT)
+        nc.vector.tensor_copy(z[1][:].indirect(take_sb[:]), given[1])
         nc.scalar.activation(z[2][:].indirect(take_sb[:, early]), given_early[:], COPY)
         nc.scalar.activation(z[3][:].indirect(take_sb[:]), given[3], COPY)
         nc.vector.tensor_copy(z[2][:].indirect(take_sb[:, late]), given_late[:])
 
         chunks = [slice(c * CHUNK, (c + 1) * CHUNK) for c in range(S // CHUNK)]
-        rounded = shared.tile([P, PACK, S], BF16, name="rounded", offset=7 * V * 2, align_bytes=256)
-        nc.scalar.copy(rounded[:, 0, :], z[0][:])
-        nc.vector.tensor_copy(rounded[:, 1, :], z[1][:])
+        joined = planes[:].rearrange("p (t c) -> p t c", t=PACK)
+        nc.vector.tensor_copy(joined[:, 1, :], z[1][:])
+        nc.scalar.copy(joined[:, 2, halves[0]], z[2][:, halves[0]])
         for a in range(2):
-            for t in (2, 3):
-                nc.vector.tensor_copy(rounded[:, t, halves[a]], z[t][:, halves[a]])
+            nc.vector.tensor_copy(joined[:, 3, halves[a]], z[3][:, halves[a]])
+        nc.vector.tensor_copy(joined[:, 2, halves[1]], z[2][:, halves[1]])
 
         out_rows = out.rearrange("(m p) c -> p m c", p=P)
 
@@ -204,7 +208,7 @@ def tile_picked_ycutmix_gelu_p_kernel(tc, x_words, x_scales, w1, w2, offs, give,
         def weave(copy, c, groups):
             copy(
                 woven[c][:].rearrange("p (c i t) -> p c t i", i=PACK, t=PACK)[:, groups],
-                rounded[:, :, chunks[c]].rearrange("p t (c i) -> p c t i", i=PACK)[:, groups],
+                joined[:, :, chunks[c]].rearrange("p t (c i) -> p c t i", i=PACK)[:, groups],
             )
 
         def second_product(c, z_codes, z_scales):

@@ -37,7 +37,7 @@ def tile_picked_ycutmix_gelu_p_kernel(tc, x_words, x_scales, w1, w2, offs, give,
         psum = ctx.enter_context(tc.psum_pool(name="psum", bufs=1))
 
         def sb(name, shape, dtype, tag=None):
-            return keep.tile(shape, dtype, name=name, tag=tag or name, align_bytes=256)
+            return keep.tile(shape, dtype, name=name, tag=tag or name, align_bytes=1024)
 
         halves = [slice(0, HALF), slice(HALF, S)]
 

@@ -42,9 +42,9 @@ def tile_picked_ycutmix_gelu_p_kernel(tc, x_words, x_scales, w1, w2, offs, give,
         halves = [slice(0, HALF), slice(HALF, S)]
 
         scale_rows = sb("scale_rows", [P, T], U8)
-        nc.vector.memset(scale_rows[:].bitcast(I32), 0)
+        nc.gpsimd.memset(scale_rows[:].bitcast(I32), 0)
         x_scale = sb("x_scale", [P, PASSES, S], U8)
-        nc.vector.memset(x_scale[:].rearrange("p o c -> p (o c)").bitcast(I32), 0)
+        nc.gpsimd.memset(x_scale[:].rearrange("p o c -> p (o c)").bitcast(I32), 0)
 
         w1_raw = [sb(f"w1_raw{o}", [P, PACK, H], F32) for o in range(PASSES)]
         offs_sb = lists.tile([P, S // LIST_ROWS], U16, name="offs_sb")

@@ -171,9 +171,7 @@ def tile_picked_ycutmix_gelu_p_kernel(tc, x_words, x_scales, w1, w2, offs, give,
         ones = shared.tile([P, V], F32, name="ones", offset=N * PACK * 2 + PACK * S * 4, align_bytes=256)
         nc.gpsimd.memset(ones[:], 1.0)
         z = [planes[:, 0:S]] + [sb(f"z{t}", [P, S], F32)[:] for t in range(1, PACK)]
-        given = {t: shared.tile([P, V], F32, name=f"given{t}", offset=i * V * 4, align_bytes=256)[:] for i, t in enumerate((0, 1, 3))}
-        given_late = shared.tile([P, V // 2], F32, name="given_late", offset=3 * V * 4, align_bytes=256)
-        given_early = shared.tile([P, V // 2], F32, name="given_early", offset=7 * V * 2, align_bytes=256)
+        given = {t: shared.tile([P, V], F32, name=f"given{t}", offset=i * V * 4, align_bytes=256)[:] for i, t in enumerate(range(PACK))}
         early, late = slice(0, V // LIST_ROWS // 2), slice(V // LIST_ROWS // 2, V // LIST_ROWS)
         for i, bank in enumerate(banks):
             if bank[0][0] == bank[-1][0]:
@@ -184,14 +182,13 @@ def tile_picked_ycutmix_gelu_p_kernel(tc, x_words, x_scales, w1, w2, offs, give,
 
         for t in (0, 1):
             nc.vector.tensor_copy(given[t], z[t][:].indirect(give_sb[:]))
-        nc.scalar.activation(given_early[:], z[2][:].indirect(give_sb[:, early]), COPY)
-        nc.scalar.activation(given_late[:], z[2][:].indirect(give_sb[:, late]), COPY)
-        nc.scalar.activation(given[3], z[3][:].indirect(give_sb[:]), COPY)
+        for t in (2, 3):
+            nc.scalar.activation(given[t], z[t][:].indirect(give_sb[:]), COPY)
         nc.vector.tensor_tensor(planes[:].indirect(take_sb[:]), given[0], ones[:], MULT)
         nc.vector.tensor_copy(z[1][:].indirect(take_sb[:]), given[1])
-        nc.scalar.activation(z[2][:].indirect(take_sb[:, early]), given_early[:], COPY)
+        nc.scalar.activation(z[2][:].indirect(take_sb[:, early]), given[2][:, : V // 2], COPY)
         nc.scalar.activation(z[3][:].indirect(take_sb[:]), given[3], COPY)
-        nc.vector.tensor_copy(z[2][:].indirect(take_sb[:, late]), given_late[:])
+        nc.vector.tensor_copy(z[2][:].indirect(take_sb[:, late]), given[2][:, V // 2 :])
 
         chunks = [slice(c * CHUNK, (c + 1) * CHUNK) for c in range(S // CHUNK)]
         joined = planes[:].rearrange("p (t c) -> p t c", t=PACK)

@@ -22,8 +22,7 @@ K_PASS = P * PACK
 PASSES = K // K_PASS
 HALF = S // 2
 LIST_ROWS = 16
-GROUPS = H // (PACK * PACK)
-VECTOR_SHARE = 16
+VECTOR_SHARE = 32
 CHUNK = 128
 SPREAD = 4
 
@@ -84,11 +83,11 @@ def tile_picked_ycutmix_gelu_p_kernel(tc, x_words, x_scales, w1, w2, offs, give,
         for o, q in places[5:]:
             place_scale_rows(o, q)
 
-        def round_w1(copy, o, values, planes, groups):
-            dst = values[:].rearrange("p (t g c j) -> p t g j c", g=GROUPS, c=PACK, j=PACK)
-            src = w1_raw[o][:].rearrange("p j (g t c) -> p t g j c", t=PACK, c=PACK)
-            first = planes.start % dst.shape[1]
-            copy(dst[:, first : first + planes.stop - planes.start, groups], src[:, planes, groups])
+        def round_w1(copy, o, values, planes, rows):
+            count = planes.stop - planes.start
+            dst = values[:].rearrange("p (t m j) -> p m j t", t=count, j=PACK)
+            src = w1_raw[o][:].rearrange("p j (m t) -> p m j t", t=PACK)
+            copy(dst[:, rows], src[:, rows, :, planes])
 
         def quantise(name, values, tag=None):
             width = values.shape[1] // PACK
@@ -136,20 +135,18 @@ def tile_picked_ycutmix_gelu_p_kernel(tc, x_words, x_scales, w1, w2, offs, give,
         def by_plane(codes, scales):
             return [(codes[:, t * P : (t + 1) * P], scales[:, t * P : (t + 1) * P]) for t in range(codes.shape[1] // P)]
 
-        every = slice(0, GROUPS)
+        every = slice(0, P)
         w1_bf = sb("w1_bf0", [P, H * PACK], BF16)
         round_w1(nc.scalar.copy, 0, w1_bf, slice(0, PACK), every)
         w1_mx = [by_plane(*quantise("w1_0", w1_bf[:]))]
         w2_raw = sb("w2_raw", [P, PACK, N], F32, tag="w1_raw0")
-        for t in range(PACK):
-            nc.sync.dma_start(w2_raw[:, t, :], w2.rearrange("(g t c) n -> t g c n", t=PACK, c=PACK)[t])
+        nc.sync.dma_start(w2_raw[:], w2.rearrange("(p t) n -> p t n", t=PACK))
         x_codes = [pick_words(0, None, halves)]
         low = sb("w1_low", [P, H * PACK // 2], BF16)
         high = sb("w1_high", [P, H * PACK // 2], BF16)
         round_w1(nc.vector.tensor_copy, 1, low, slice(0, 2), every)
-        round_w1(nc.vector.tensor_copy, 1, high, slice(2, 3), slice(0, VECTOR_SHARE))
-        round_w1(nc.scalar.copy, 1, high, slice(3, 4), every)
-        round_w1(nc.scalar.copy, 1, high, slice(2, 3), slice(VECTOR_SHARE, GROUPS))
+        round_w1(nc.vector.tensor_copy, 1, high, slice(2, 4), slice(0, VECTOR_SHARE))
+        round_w1(nc.scalar.copy, 1, high, slice(2, 4), slice(VECTOR_SHARE, P))
         w1_mx.append(by_plane(*quantise("w1_low", low[:])) + by_plane(*quantise("w1_high", high[:])))
         x_codes.append(pick_words(1, None, (first, middle, last)))
         for o in range(PASSES):

@@ -140,7 +140,8 @@ def tile_picked_ycutmix_gelu_p_kernel(tc, x_words, x_scales, w1, w2, offs, give,
         round_w1(nc.scalar.copy, 0, w1_bf, slice(0, PACK), every)
         w1_mx = [by_plane(*quantise("w1_0", w1_bf[:]))]
         w2_raw = sb("w2_raw", [P, PACK, N], F32, tag="w1_raw0")
-        nc.sync.dma_start(w2_raw[:], w2.rearrange("(p t) n -> p t n", t=PACK))
+        for c in range(SPREAD):
+            nc.sync.dma_start(w2_raw[c:P:SPREAD], w2.rearrange("(g c t) n -> c g t n", c=SPREAD, t=PACK)[c])
         x_codes = [pick_words(0, None, halves)]
         low = sb("w1_low", [P, H * PACK // 2], BF16)
         high = sb("w1_high", [P, H * PACK // 2], BF16)

@@ -33,6 +33,7 @@ def tile_picked_ycutmix_gelu_p_kernel(tc, x_words, x_scales, w1, w2, offs, give,
         lists = ctx.enter_context(tc.tile_pool(name="lists", bufs=1))
         keep = ctx.enter_context(tc.tile_pool(name="keep", bufs=1))
         shared = ctx.enter_context(tc.tile_pool(name="shared", bufs=1))
+        reused = ctx.enter_context(tc.tile_pool(name="reused", bufs=1))
         psum = ctx.enter_context(tc.psum_pool(name="psum", bufs=1))
 
         def sb(name, shape, dtype, tag=None):
@@ -45,7 +46,7 @@ def tile_picked_ycutmix_gelu_p_kernel(tc, x_words, x_scales, w1, w2, offs, give,
         x_scale = sb("x_scale", [P, PASSES, S], U8)
         nc.gpsimd.memset(x_scale[:].rearrange("p o c -> p (o c)").bitcast(I32), 0)
 
-        w1_raw = [sb(f"w1_raw{o}", [P, PACK, H], F32) for o in range(PASSES)]
+        w1_raw = [reused.tile([P, PACK, H], F32, name="w1_raw0", offset=0, align_bytes=1024), sb("w1_raw1", [P, PACK, H], F32)]
         offs_sb = lists.tile([P, S // LIST_ROWS], U16, name="offs_sb")
         give_sb = lists.tile([P, V // LIST_ROWS], U16, name="give_sb")
         take_sb = lists.tile([P, V // LIST_ROWS], U16, name="take_sb")
@@ -139,7 +140,7 @@ def tile_picked_ycutmix_gelu_p_kernel(tc, x_words, x_scales, w1, w2, offs, give,
         w1_bf = sb("w1_bf0", [P, H * PACK], BF16)
         round_w1(nc.scalar.copy, 0, w1_bf, slice(0, PACK), every)
         w1_mx = [by_plane(*quantise("w1_0", w1_bf[:]))]
-        w2_raw = sb("w2_raw", [P, PACK, N], F32, tag="w1_raw0")
+        w2_raw = reused.tile([P, PACK, N], F32, name="w2_raw", offset=0, align_bytes=1024)
         for c in range(SPREAD):
             nc.sync.dma_start(w2_raw[c:P:SPREAD], w2.rearrange("(g c t) n -> c g t n", c=SPREAD, t=PACK)[c])
         x_codes = [pick_words(0, None, halves)]
@@ -153,23 +154,24 @@ def tile_picked_ycutmix_gelu_p_kernel(tc, x_words, x_scales, w1, w2, offs, give,
         for o in range(PASSES):
             first_product(o)
 
-        w2_bf = shared.tile([P, N * PACK], BF16, name="w2_bf", offset=0, align_bytes=256)
+        w2_bf = [shared.tile([P, P * PACK], BF16, name=f"w2_bf{m}", offset=m * P * PACK * 2, align_bytes=256) for m in range(N // P)]
         w2_codes = sb("w2_codes", [P, N], U32)
         w2_scales = sb("w2_scales", [P, N], U8)
         blocks = [slice(m * P, (m + 1) * P) for m in range(N // P)]
         for m in range(N // P):
             nc.vector.tensor_copy(
-                w2_bf[:, m * P * PACK : (m + 1) * P * PACK].rearrange("p (c i j) -> p c j i", i=PACK, j=PACK),
+                w2_bf[m][:].rearrange("p (c i j) -> p c j i", i=PACK, j=PACK),
                 w2_raw[:, :, blocks[m]].rearrange("p j (c i) -> p c j i", i=PACK),
             )
         for m in range(N // P):
-            nc.vector.quantize_mx(out=w2_codes[:, blocks[m]].bitcast(FP8X4), scales=w2_scales[:, blocks[m]], in_=w2_bf[:, m * P * PACK : (m + 1) * P * PACK])
+            nc.vector.quantize_mx(out=w2_codes[:, blocks[m]].bitcast(FP8X4), scales=w2_scales[:, blocks[m]], in_=w2_bf[m][:])
 
         planes = shared.tile([P, PACK * S], F32, name="planes", offset=N * PACK * 2, align_bytes=256)
         ones = shared.tile([P, V], F32, name="ones", offset=N * PACK * 2 + PACK * S * 4, align_bytes=256)
-        nc.gpsimd.memset(ones[:], 1.0)
+        nc.vector.memset(ones[:], 1.0)
         z = [planes[:, 0:S]] + [sb(f"z{t}", [P, S], F32)[:] for t in range(1, PACK)]
-        given = {t: shared.tile([P, V], F32, name=f"given{t}", offset=i * V * 4, align_bytes=256)[:] for i, t in enumerate(range(PACK))}
+        given = [reused.tile([P, V], F32, name=f"given{t}", offset=t * 1024, align_bytes=1024)[:] for t in (0, 1)]
+        given = given + [shared.tile([P, V], F32, name=f"given{t}", offset=(t - 2) * V * 4, align_bytes=256)[:] for t in (2, 3)]
         early, late = slice(0, V // LIST_ROWS // 2), slice(V // LIST_ROWS // 2, V // LIST_ROWS)
         for i, bank in enumerate(banks):
             if bank[0][0] == bank[-1][0]:
@@ -190,11 +192,10 @@ def tile_picked_ycutmix_gelu_p_kernel(tc, x_words, x_scales, w1, w2, offs, give,
 
         chunks = [slice(c * CHUNK, (c + 1) * CHUNK) for c in range(S // CHUNK)]
         joined = planes[:].rearrange("p (t c) -> p t c", t=PACK)
-        nc.vector.tensor_copy(joined[:, 1, :], z[1][:])
-        nc.scalar.copy(joined[:, 2, halves[0]], z[2][:, halves[0]])
-        for a in range(2):
-            nc.vector.tensor_copy(joined[:, 3, halves[a]], z[3][:, halves[a]])
-        nc.vector.tensor_copy(joined[:, 2, halves[1]], z[2][:, halves[1]])
+        for t in (1, 2, 3):
+            nc.scalar.copy(joined[:, t, chunks[0]], z[t][:, chunks[0]])
+        for t, cols in ((1, slice(CHUNK, S)), (2, slice(CHUNK, S)), (3, chunks[1]), (3, halves[1])):
+            nc.vector.tensor_copy(joined[:, t, cols], z[t][:, cols])
 
         out_rows = out.rearrange("(m p) c -> p m c", p=P)
 
@@ -206,12 +207,12 @@ def tile_picked_ycutmix_gelu_p_kernel(tc, x_words, x_scales, w1, w2, offs, give,
                 joined[:, :, chunks[c]].rearrange("p t (c i) -> p c t i", i=PACK)[:, groups],
             )
 
-        def second_product(c, z_codes, z_scales):
-            last = c == len(chunks) - 1
+        def second_product(step, c, z_codes, z_scales):
+            last = step == len(chunks) - 1
             if last:
-                res = [psum.tile([P, CHUNK], F32, name=f"res{c}_{m}", tag=f"bank{c + m}")[:] for m in range(N // P)]
+                res = [psum.tile([P, CHUNK], F32, name=f"res{c}_{m}", tag=f"bank{step + m}")[:] for m in range(N // P)]
             else:
-                bank = psum.tile([P, N // P, CHUNK], F32, name=f"res{c}", tag=f"bank{c}")
+                bank = psum.tile([P, N // P, CHUNK], F32, name=f"res{c}", tag=f"bank{step}")
                 res = [bank[:, m, :] for m in range(N // P)]
             for m in range(N // P):
                 nc.tensor.matmul_mx(
@@ -228,14 +229,15 @@ def tile_picked_ycutmix_gelu_p_kernel(tc, x_words, x_scales, w1, w2, offs, give,
                 nc.vector.tensor_copy(staged[:, 0, :], res[0])
                 nc.scalar.copy(staged[:, 1, :], res[1])
             else:
-                copy = nc.scalar.copy if c < 2 else nc.vector.tensor_copy
+                copy = nc.scalar.copy if step < 2 else nc.vector.tensor_copy
                 copy(staged[:], bank[:])
-            queue = nc.scalar if c % 2 else nc.sync
+            queue = nc.scalar if step % 2 else nc.sync
             queue.dma_start(out_rows[:, :, chunks[c]], staged[:])
 
         groups = CHUNK // PACK
         for c in range(len(chunks)):
-            weave(nc.scalar.copy if c % 2 else nc.vector.tensor_copy, c, slice(0, groups))
-        z_mx = [quantise(f"z{c}", woven[c][:]) for c in range(len(chunks))]
-        for c in range(len(chunks)):
-            second_product(c, *z_mx[c])
+            weave(nc.vector.tensor_copy if c in (1, 2) else nc.scalar.copy, c, slice(0, groups))
+        order = (1, 0, 2, 3)
+        z_mx = [quantise(f"z{c}", woven[c][:]) for c in order]
+        for step, c in enumerate(order):
+            second_product(step, c, *z_mx[step])

@@ -141,8 +141,8 @@ def tile_picked_ycutmix_gelu_p_kernel(tc, x_words, x_scales, w1, w2, offs, give,
         round_w1(nc.scalar.copy, 0, w1_bf, slice(0, PACK), every)
         w1_mx = [by_plane(*quantise("w1_0", w1_bf[:]))]
         w2_raw = reused.tile([P, PACK, N], F32, name="w2_raw", offset=0, align_bytes=1024)
-        for c in range(SPREAD):
-            nc.sync.dma_start(w2_raw[c:P:SPREAD], w2.rearrange("(g c t) n -> c g t n", c=SPREAD, t=PACK)[c])
+        for start, step in ((0, 2), (1, 4), (3, 4)):
+            nc.sync.dma_start(w2_raw[start:P:step], w2.rearrange("(g c t) n -> c g t n", c=step, t=PACK)[start])
         x_codes = [pick_words(0, None, halves)]
         low = sb("w1_low", [P, H * PACK // 2], BF16)
         high = sb("w1_high", [P, H * PACK // 2], BF16)
@@ -207,6 +207,8 @@ def tile_picked_ycutmix_gelu_p_kernel(tc, x_words, x_scales, w1, w2, offs, give,
                 joined[:, :, chunks[c]].rearrange("p t (c i) -> p c t i", i=PACK)[:, groups],
             )
 
+        staged = sb("staged", [P, N // P, S], F32)
+
         def second_product(step, c, z_codes, z_scales):
             last = step == len(chunks) - 1
             if last:
@@ -224,15 +226,18 @@ def tile_picked_ycutmix_gelu_p_kernel(tc, x_words, x_scales, w1, w2, offs, give,
                     start=True,
                     stop=True,
                 )
-            staged = sb(f"staged{c}", [P, N // P, CHUNK], F32)
             if last:
-                nc.vector.tensor_copy(staged[:, 0, :], res[0])
-                nc.scalar.copy(staged[:, 1, :], res[1])
+                nc.scalar.copy(staged[:, 0, chunks[c]], res[0])
+                nc.scalar.dma_start(out_rows[:, 0, chunks[c]], staged[:, 0, chunks[c]])
+                nc.vector.tensor_copy(staged[:, 1, chunks[c]], res[1])
+                nc.sync.dma_start(out_rows[:, 1, chunks[c]], staged[:, 1, chunks[c]])
+            elif step == 2:
+                nc.vector.tensor_copy(staged[:, :, chunks[c]], bank[:])
+                nc.sync.dma_start(out_rows[:, :, chunks[c]], staged[:, :, chunks[c]])
             else:
-                copy = nc.scalar.copy if step < 2 else nc.vector.tensor_copy
-                copy(staged[:], bank[:])
-            queue = nc.scalar if step % 2 else nc.sync
-            queue.dma_start(out_rows[:, :, chunks[c]], staged[:])
+                nc.scalar.copy(staged[:, :, chunks[c]], bank[:])
+                queue = nc.scalar if step else nc.sync
+                queue.dma_start(out_rows[:, :, chunks[c]], staged[:, :, chunks[c]])
 
         groups = CHUNK // PACK
         for c in range(len(chunks)):

@@ -141,7 +141,7 @@ def tile_picked_ycutmix_gelu_p_kernel(tc, x_words, x_scales, w1, w2, offs, give,
         round_w1(nc.scalar.copy, 0, w1_bf, slice(0, PACK), every)
         w1_mx = [by_plane(*quantise("w1_0", w1_bf[:]))]
         w2_raw = reused.tile([P, PACK, N], F32, name="w2_raw", offset=0, align_bytes=1024)
-        for start, step in ((0, 2), (1, 4), (3, 4)):
+        for start, step in ((0, 2), (1, 2)):
             nc.sync.dma_start(w2_raw[start:P:step], w2.rearrange("(g c t) n -> c g t n", c=step, t=PACK)[start])
         x_codes = [pick_words(0, None, halves)]
         low = sb("w1_low", [P, H * PACK // 2], BF16)
@@ -210,9 +210,9 @@ def tile_picked_ycutmix_gelu_p_kernel(tc, x_words, x_scales, w1, w2, offs, give,
         staged = sb("staged", [P, N // P, S], F32)
 
         def second_product(step, c, z_codes, z_scales):
-            last = step == len(chunks) - 1
-            if last:
-                res = [psum.tile([P, CHUNK], F32, name=f"res{c}_{m}", tag=f"bank{step + m}")[:] for m in range(N // P)]
+            split = step in (0, len(chunks) - 1)
+            if split:
+                res = [psum.tile([P, CHUNK], F32, name=f"res{c}_{m}", tag=f"bank{step + 4 * m}")[:] for m in range(N // P)]
             else:
                 bank = psum.tile([P, N // P, CHUNK], F32, name=f"res{c}", tag=f"bank{step}")
                 res = [bank[:, m, :] for m in range(N // P)]
@@ -226,18 +226,21 @@ def tile_picked_ycutmix_gelu_p_kernel(tc, x_words, x_scales, w1, w2, offs, give,
                     start=True,
                     stop=True,
                 )
-            if last:
-                nc.scalar.copy(staged[:, 0, chunks[c]], res[0])
-                nc.scalar.dma_start(out_rows[:, 0, chunks[c]], staged[:, 0, chunks[c]])
-                nc.vector.tensor_copy(staged[:, 1, chunks[c]], res[1])
-                nc.sync.dma_start(out_rows[:, 1, chunks[c]], staged[:, 1, chunks[c]])
+            if step == 0:
+                for m in range(N // P):
+                    nc.scalar.copy(staged[:, m, chunks[c]], res[m])
+                    nc.sync.dma_start(out_rows[:, m, chunks[c]], staged[:, m, chunks[c]])
+            elif step == 1:
+                nc.scalar.copy(staged[:, :, chunks[c]], bank[:])
+                nc.scalar.dma_start(out_rows[:, :, chunks[c]], staged[:, :, chunks[c]])
             elif step == 2:
                 nc.vector.tensor_copy(staged[:, :, chunks[c]], bank[:])
                 nc.sync.dma_start(out_rows[:, :, chunks[c]], staged[:, :, chunks[c]])
             else:
-                nc.scalar.copy(staged[:, :, chunks[c]], bank[:])
-                queue = nc.scalar if step else nc.sync
-                queue.dma_start(out_rows[:, :, chunks[c]], staged[:, :, chunks[c]])
+                nc.scalar.copy(staged[:, 0, chunks[c]], res[0])
+                nc.scalar.dma_start(out_rows[:, 0, chunks[c]], staged[:, 0, chunks[c]])
+                nc.vector.tensor_copy(staged[:, 1, chunks[c]], res[1])
+                nc.sync.dma_start(out_rows[:, 1, chunks[c]], staged[:, 1, chunks[c]])
 
         groups = CHUNK // PACK
         for c in range(len(chunks)):

@@ -211,14 +211,10 @@ def tile_picked_ycutmix_gelu_p_kernel(tc, x_words, x_scales, w1, w2, offs, give,
 
         def second_product(step, c, z_codes, z_scales):
             split = step in (0, len(chunks) - 1)
-            if split:
-                res = [psum.tile([P, CHUNK], F32, name=f"res{c}_{m}", tag=f"bank{step + 4 * m}")[:] for m in range(N // P)]
-            else:
-                bank = psum.tile([P, N // P, CHUNK], F32, name=f"res{c}", tag=f"bank{step}")
-                res = [bank[:, m, :] for m in range(N // P)]
             for m in range(N // P):
+                bank = psum.tile([P, CHUNK], F32, name=f"res{c}_{m}", tag=f"bank{2 * step + m}")
                 nc.tensor.matmul_mx(
-                    out=res[m],
+                    out=bank[:],
                     lhsT=w2_codes[:, m * P : (m + 1) * P].bitcast(FP8X4),
                     lhsT_scale=w2_scales[:, m * P : (m + 1) * P],
                     rhs=z_codes[:].bitcast(FP8X4),
@@ -226,21 +222,12 @@ def tile_picked_ycutmix_gelu_p_kernel(tc, x_words, x_scales, w1, w2, offs, give,
                     start=True,
                     stop=True,
                 )
-            if step == 0:
-                for m in range(N // P):
-                    nc.scalar.copy(staged[:, m, chunks[c]], res[m])
+                copy = nc.vector.tensor_copy if step > 1 and m == 0 else nc.scalar.copy
+                copy(staged[:, m, chunks[c]], bank[:])
+                if split:
                     nc.sync.dma_start(out_rows[:, m, chunks[c]], staged[:, m, chunks[c]])
-            elif step == 1:
-                nc.scalar.copy(staged[:, :, chunks[c]], bank[:])
-                nc.scalar.dma_start(out_rows[:, :, chunks[c]], staged[:, :, chunks[c]])
-            elif step == 2:
-                nc.vector.tensor_copy(staged[:, :, chunks[c]], bank[:])
+            if not split:
                 nc.sync.dma_start(out_rows[:, :, chunks[c]], staged[:, :, chunks[c]])
-            else:
-                nc.scalar.copy(staged[:, 0, chunks[c]], res[0])
-                nc.scalar.dma_start(out_rows[:, 0, chunks[c]], staged[:, 0, chunks[c]])
-                nc.vector.tensor_copy(staged[:, 1, chunks[c]], res[1])
-                nc.sync.dma_start(out_rows[:, 1, chunks[c]], staged[:, 1, chunks[c]])
 
         groups = CHUNK // PACK
         for c in range(len(chunks)):

@@ -141,7 +141,7 @@ def tile_picked_ycutmix_gelu_p_kernel(tc, x_words, x_scales, w1, w2, offs, give,
         round_w1(nc.scalar.copy, 0, w1_bf, slice(0, PACK), every)
         w1_mx = [by_plane(*quantise("w1_0", w1_bf[:]))]
         w2_raw = reused.tile([P, PACK, N], F32, name="w2_raw", offset=0, align_bytes=1024)
-        for start, step in ((0, 2), (1, 2)):
+        for start, step in ((0, 2), (1, 4), (3, 4)):
             nc.sync.dma_start(w2_raw[start:P:step], w2.rearrange("(g c t) n -> c g t n", c=step, t=PACK)[start])
         x_codes = [pick_words(0, None, halves)]
         low = sb("w1_low", [P, H * PACK // 2], BF16)
@@ -210,7 +210,7 @@ def tile_picked_ycutmix_gelu_p_kernel(tc, x_words, x_scales, w1, w2, offs, give,
         staged = sb("staged", [P, N // P, S], F32)
 
         def second_product(step, c, z_codes, z_scales):
-            split = step in (0, len(chunks) - 1)
+            split = step == 0
             for m in range(N // P):
                 bank = psum.tile([P, CHUNK], F32, name=f"res{c}_{m}", tag=f"bank{2 * step + m}")
                 nc.tensor.matmul_mx(
@@ -222,7 +222,7 @@ def tile_picked_ycutmix_gelu_p_kernel(tc, x_words, x_scales, w1, w2, offs, give,
                     start=True,
                     stop=True,
                 )
-                copy = nc.vector.tensor_copy if step > 1 and m == 0 else nc.scalar.copy
+                copy = nc.vector.tensor_copy if step == 2 else nc.scalar.copy
                 copy(staged[:, m, chunks[c]], bank[:])
                 if split:
                     nc.sync.dma_start(out_rows[:, m, chunks[c]], staged[:, m, chunks[c]])

@@ -141,8 +141,8 @@ def tile_picked_ycutmix_gelu_p_kernel(tc, x_words, x_scales, w1, w2, offs, give,
         round_w1(nc.scalar.copy, 0, w1_bf, slice(0, PACK), every)
         w1_mx = [by_plane(*quantise("w1_0", w1_bf[:]))]
         w2_raw = reused.tile([P, PACK, N], F32, name="w2_raw", offset=0, align_bytes=1024)
-        for start, step in ((0, 2), (1, 4), (3, 4)):
-            nc.sync.dma_start(w2_raw[start:P:step], w2.rearrange("(g c t) n -> c g t n", c=step, t=PACK)[start])
+        for rows in (slice(0, 2), slice(2, 3), slice(3, 4)):
+            nc.sync.dma_start(w2_raw[:, rows], w2.rearrange("(p t) n -> p t n", t=PACK)[:, rows])
         x_codes = [pick_words(0, None, halves)]
         low = sb("w1_low", [P, H * PACK // 2], BF16)
         high = sb("w1_high", [P, H * PACK // 2], BF16)

@@ -51,21 +51,22 @@ def tile_picked_ycutmix_gelu_p_kernel(tc, x_words, x_scales, w1, w2, offs, give,
         give_sb = lists.tile([P, V // LIST_ROWS], U16, name="give_sb")
         take_sb = lists.tile([P, V // LIST_ROWS], U16, name="take_sb")
 
-        def load_w1(o):
-            nc.sync.dma_start(w1_raw[o][:], w1[o * K_PASS : (o + 1) * K_PASS, :].rearrange("(p j) c -> p j c", j=PACK))
+        def load_w1(o, rows):
+            nc.sync.dma_start(w1_raw[o][:, rows], w1[o * K_PASS : (o + 1) * K_PASS, :].rearrange("(p j) c -> p j c", j=PACK)[:, rows])
 
         def load_words(o, tag=None):
             table = sb(f"x_tab{o}", [P, T], U32, tag=tag)
             nc.sync.dma_start(table[:].bitcast(I32), x_words[o].rearrange("p c r -> p (c r)").bitcast(I32))
             return table
 
-        load_w1(0)
+        load_w1(0, slice(0, 2))
         nc.sync.dma_start(scale_rows[0:P:SPREAD, :].bitcast(I32), x_scales.rearrange("o q c -> (o q) c").bitcast(I32))
         nc.sync.dma_start(offs_sb[:], offs)
+        load_w1(0, slice(2, 4))
         nc.sync.dma_start(give_sb[:], give)
         nc.sync.dma_start(take_sb[:], take)
         x_tab = [load_words(0)]
-        load_w1(1)
+        load_w1(1, slice(0, 4))
 
         picked_rows = sb("picked_rows", [P, S], U8)
         nc.vector.tensor_copy(picked_rows[:], scale_rows[:].indirect(offs_sb[:]))
@@ -138,11 +139,11 @@ def tile_picked_ycutmix_gelu_p_kernel(tc, x_words, x_scales, w1, w2, offs, give,
 
         every = slice(0, P)
         w1_bf = sb("w1_bf0", [P, H * PACK], BF16)
-        round_w1(nc.scalar.copy, 0, w1_bf, slice(0, PACK), every)
+        round_w1(nc.vector.tensor_copy, 0, w1_bf, slice(0, PACK), every)
         w1_mx = [by_plane(*quantise("w1_0", w1_bf[:]))]
         w2_raw = reused.tile([P, PACK, N], F32, name="w2_raw", offset=0, align_bytes=1024)
-        for rows in (slice(0, 2), slice(2, 3), slice(3, 4)):
-            nc.sync.dma_start(w2_raw[:, rows], w2.rearrange("(p t) n -> p t n", t=PACK)[:, rows])
+        for e in range(2):
+            nc.sync.dma_start(w2_raw[e:P:2], w2.rearrange("(g e t) n -> e g t n", e=2, t=PACK)[e])
         x_codes = [pick_words(0, None, halves)]
         low = sb("w1_low", [P, H * PACK // 2], BF16)
         high = sb("w1_high", [P, H * PACK // 2], BF16)
@@ -194,7 +195,7 @@ def tile_picked_ycutmix_gelu_p_kernel(tc, x_words, x_scales, w1, w2, offs, give,
         joined = planes[:].rearrange("p (t c) -> p t c", t=PACK)
         for t in (1, 2, 3):
             nc.scalar.copy(joined[:, t, chunks[0]], z[t][:, chunks[0]])
-        for t, cols in ((1, slice(CHUNK, S)), (2, slice(CHUNK, S)), (3, chunks[1]), (3, halves[1])):
+        for t, cols in ((1, slice(CHUNK, S)), (2, chunks[1]), (3, chunks[1]), (2, halves[1]), (3, halves[1])):
             nc.vector.tensor_copy(joined[:, t, cols], z[t][:, cols])
 
         out_rows = out.rearrange("(m p) c -> p m c", p=P)
@@ -232,7 +233,7 @@ def tile_picked_ycutmix_gelu_p_kernel(tc, x_words, x_scales, w1, w2, offs, give,
         groups = CHUNK // PACK
         for c in range(len(chunks)):
             weave(nc.vector.tensor_copy if c in (1, 2) else nc.scalar.copy, c, slice(0, groups))
-        order = (1, 0, 2, 3)
+        order = (1, 2, 0, 3)
         z_mx = [quantise(f"z{c}", woven[c][:]) for c in order]
         for step, c in enumerate(order):
             second_product(step, c, *z_mx[step])

from contextlib import ExitStack

import concourse.mybir as mybir

K, T, S, H, N, V = 1024, 2048, 512, 512, 256, 128
FLOPS = 2 * K * H * S + 2 * H * N * S

F32 = mybir.dt.float32
BF16 = mybir.dt.bfloat16
I32 = mybir.dt.int32
U32 = mybir.dt.uint32
U16 = mybir.dt.uint16
U8 = mybir.dt.uint8
FP8X4 = mybir.dt.float8_e4m3fn_x4
GELU = mybir.ActivationFunctionType.Gelu_apprx_tanh
COPY = mybir.ActivationFunctionType.Copy
MULT = mybir.AluOpType.mult

P = 128
PACK = 4
K_PASS = P * PACK
PASSES = K // K_PASS
HALF = S // 2
LIST_ROWS = 16
VECTOR_SHARE = 32
CHUNK = 128
SPREAD = 4


def tile_picked_ycutmix_gelu_p_kernel(tc, x_words, x_scales, w1, w2, offs, give, take, out):
    nc = tc.nc
    with ExitStack() as ctx:
        lists = ctx.enter_context(tc.tile_pool(name="lists", bufs=1))
        keep = ctx.enter_context(tc.tile_pool(name="keep", bufs=1))
        shared = ctx.enter_context(tc.tile_pool(name="shared", bufs=1))
        reused = ctx.enter_context(tc.tile_pool(name="reused", bufs=1))
        psum = ctx.enter_context(tc.psum_pool(name="psum", bufs=1))

        def sb(name, shape, dtype, tag=None):
            return keep.tile(shape, dtype, name=name, tag=tag or name, align_bytes=1024)

        halves = [slice(0, HALF), slice(HALF, S)]

        scale_rows = sb("scale_rows", [P, T], U8)
        nc.gpsimd.memset(scale_rows[:].bitcast(I32), 0)
        x_scale = sb("x_scale", [P, PASSES, S], U8)
        nc.gpsimd.memset(x_scale[:].rearrange("p o c -> p (o c)").bitcast(I32), 0)

        w1_raw = [reused.tile([P, PACK, H], F32, name="w1_raw0", offset=0, align_bytes=1024), sb("w1_raw1", [P, PACK, H], F32)]
        offs_sb = lists.tile([P, S // LIST_ROWS], U16, name="offs_sb")
        give_sb = lists.tile([P, V // LIST_ROWS], U16, name="give_sb")
        take_sb = lists.tile([P, V // LIST_ROWS], U16, name="take_sb")

        def load_w1(o, rows):
            nc.sync.dma_start(w1_raw[o][:, rows], w1[o * K_PASS : (o + 1) * K_PASS, :].rearrange("(p j) c -> p j c", j=PACK)[:, rows])

        def load_words(o, tag=None):
            table = sb(f"x_tab{o}", [P, T], U32, tag=tag)
            nc.sync.dma_start(table[:].bitcast(I32), x_words[o].rearrange("p c r -> p (c r)").bitcast(I32))
            return table

        load_w1(0, slice(0, 2))
        nc.sync.dma_start(scale_rows[0:P:SPREAD, :].bitcast(I32), x_scales.rearrange("o q c -> (o q) c").bitcast(I32))
        nc.sync.dma_start(offs_sb[:], offs)
        load_w1(0, slice(2, 4))
        nc.sync.dma_start(give_sb[:], give)
        nc.sync.dma_start(take_sb[:], take)
        x_tab = [load_words(0)]
        load_w1(1, slice(0, 4))

        picked_rows = sb("picked_rows", [P, S], U8)
        nc.vector.tensor_copy(picked_rows[:], scale_rows[:].indirect(offs_sb[:]))

        def place_scale_rows(o, q):
            first = SPREAD * (16 * o + 4 * q)
            nc.sync.dma_start(
                x_scale[32 * q + 4 * o : 32 * q + 4 * o + 4, o, :].bitcast(I32),
                picked_rows[first : first + 4 * SPREAD : SPREAD, :].bitcast(I32),
            )

        places = [(o, q) for o in range(PASSES) for q in range(4)]
        for o, q in places[:5]:
            place_scale_rows(o, q)
        x_tab.append(load_words(1, tag="scale_rows"))
        for o, q in places[5:]:
            place_scale_rows(o, q)

        def round_w1(copy, o, values, planes, rows):
            count = planes.stop - planes.start
            dst = values[:].rearrange("p (t m j) -> p m j t", t=count, j=PACK)
            src = w1_raw[o][:].rearrange("p j (m t) -> p m j t", t=PACK)
            copy(dst[:, rows], src[:, rows, :, planes])

        def quantise(name, values, tag=None):
            width = values.shape[1] // PACK
            codes = sb(f"{name}_codes", [P, width], U32, tag=tag)
            scales = sb(f"{name}_scales", [P, width], U8)
            nc.vector.quantize_mx(out=codes[:].bitcast(FP8X4), scales=scales[:], in_=values)
            return codes, scales

        def pick_words(o, tag, runs):
            picked = sb(f"x_codes{o}", [P, S], U32, tag=tag)
            for cols in runs:
                nc.vector.tensor_copy(picked[:, cols], x_tab[o][:].indirect(offs_sb[:, cols.start // LIST_ROWS : cols.stop // LIST_ROWS]))
            return picked

        first, middle, last = slice(0, 128), slice(128, 384), slice(384, 512)
        banks = [
            [(0, first)],
            [(1, first)],
            [(2, first), (3, first)],
            [(0, middle)],
            [(0, last)],
            [(1, middle), (1, last)],
            [(2, middle), (2, last)],
            [(3, middle), (3, last)],
        ]
        acc = [psum.tile([P, sum(c.stop - c.start for t, c in b)], F32, name=f"acc{i}", tag=f"bank{i}") for i, b in enumerate(banks)]

        def first_product(o):
            for i, bank in enumerate(banks):
                at = 0
                for n, (t, cols) in enumerate(bank):
                    width = cols.stop - cols.start
                    w_codes, w_scales = w1_mx[o][t]
                    nc.tensor.matmul_mx(
                        out=acc[i][:, at : at + width],
                        lhsT=w_codes.bitcast(FP8X4),
                        lhsT_scale=w_scales,
                        rhs=x_codes[o][:, cols].bitcast(FP8X4),
                        rhs_scale=x_scale[4 * o : P, o, cols],
                        start=(o == 0 and n == 0),
                        stop=(o == PASSES - 1 and n == len(bank) - 1),
                    )
                    at = at + width

        def by_plane(codes, scales):
            return [(codes[:, t * P : (t + 1) * P], scales[:, t * P : (t + 1) * P]) for t in range(codes.shape[1] // P)]

        every = slice(0, P)
        w1_bf = sb("w1_bf0", [P, H * PACK], BF16)
        round_w1(nc.vector.tensor_copy, 0, w1_bf, slice(0, PACK), every)
        w1_mx = [by_plane(*quantise("w1_0", w1_bf[:]))]
        w2_raw = reused.tile([P, PACK, N], F32, name="w2_raw", offset=0, align_bytes=1024)
        for e in range(2):
            nc.sync.dma_start(w2_raw[e:P:2], w2.rearrange("(g e t) n -> e g t n", e=2, t=PACK)[e])
        x_codes = [pick_words(0, None, halves)]
        low = sb("w1_low", [P, H * PACK // 2], BF16)
        high = sb("w1_high", [P, H * PACK // 2], BF16)
        round_w1(nc.vector.tensor_copy, 1, low, slice(0, 2), every)
        round_w1(nc.vector.tensor_copy, 1, high, slice(2, 4), slice(0, VECTOR_SHARE))
        round_w1(nc.scalar.copy, 1, high, slice(2, 4), slice(VECTOR_SHARE, P))
        w1_mx.append(by_plane(*quantise("w1_low", low[:])) + by_plane(*quantise("w1_high", high[:])))
        x_codes.append(pick_words(1, None, (first, middle, last)))
        for o in range(PASSES):
            first_product(o)

        w2_bf = [shared.tile([P, P * PACK], BF16, name=f"w2_bf{m}", offset=m * P * PACK * 2, align_bytes=256) for m in range(N // P)]
        w2_codes = sb("w2_codes", [P, N], U32)
        w2_scales = sb("w2_scales", [P, N], U8)
        blocks = [slice(m * P, (m + 1) * P) for m in range(N // P)]
        for m in range(N // P):
            nc.vector.tensor_copy(
                w2_bf[m][:].rearrange("p (c i j) -> p c j i", i=PACK, j=PACK),
                w2_raw[:, :, blocks[m]].rearrange("p j (c i) -> p c j i", i=PACK),
            )
        for m in range(N // P):
            nc.vector.quantize_mx(out=w2_codes[:, blocks[m]].bitcast(FP8X4), scales=w2_scales[:, blocks[m]], in_=w2_bf[m][:])

        planes = shared.tile([P, PACK * S], F32, name="planes", offset=N * PACK * 2, align_bytes=256)
        ones = shared.tile([P, V], F32, name="ones", offset=N * PACK * 2 + PACK * S * 4, align_bytes=256)
        nc.vector.memset(ones[:], 1.0)
        z = [planes[:, 0:S]] + [sb(f"z{t}", [P, S], F32)[:] for t in range(1, PACK)]
        given = [reused.tile([P, V], F32, name=f"given{t}", offset=t * 1024, align_bytes=1024)[:] for t in (0, 1)]
        given = given + [shared.tile([P, V], F32, name=f"given{t}", offset=(t - 2) * V * 4, align_bytes=256)[:] for t in (2, 3)]
        early, late = slice(0, V // LIST_ROWS // 2), slice(V // LIST_ROWS // 2, V // LIST_ROWS)
        for i, bank in enumerate(banks):
            if bank[0][0] == bank[-1][0]:
                nc.scalar.activation(z[bank[0][0]][:, bank[0][1].start : bank[-1][1].stop], acc[i][:], GELU)
            else:
                for n, (t, cols) in enumerate(bank):
                    nc.scalar.activation(z[t][:, cols], acc[i][:, n * P : (n + 1) * P], GELU)

        for t in (0, 1):
            nc.vector.tensor_copy(given[t], z[t][:].indirect(give_sb[:]))
        for t in (2, 3):
            nc.scalar.activation(given[t], z[t][:].indirect(give_sb[:]), COPY)
        nc.vector.tensor_tensor(planes[:].indirect(take_sb[:]), given[0], ones[:], MULT)
        nc.vector.tensor_copy(z[1][:].indirect(take_sb[:]), given[1])
        nc.scalar.activation(z[2][:].indirect(take_sb[:, early]), given[2][:, : V // 2], COPY)
        nc.scalar.activation(z[3][:].indirect(take_sb[:]), given[3], COPY)
        nc.vector.tensor_copy(z[2][:].indirect(take_sb[:, late]), given[2][:, V // 2 :])

        chunks = [slice(c * CHUNK, (c + 1) * CHUNK) for c in range(S // CHUNK)]
        joined = planes[:].rearrange("p (t c) -> p t c", t=PACK)
        for t in (1, 2, 3):
            nc.scalar.copy(joined[:, t, chunks[0]], z[t][:, chunks[0]])
        for t, cols in ((1, slice(CHUNK, S)), (2, chunks[1]), (3, chunks[1]), (2, halves[1]), (3, halves[1])):
            nc.vector.tensor_copy(joined[:, t, cols], z[t][:, cols])

        out_rows = out.rearrange("(m p) c -> p m c", p=P)

        woven = [sb(f"z_bf{c}", [P, CHUNK * PACK], BF16) for c in range(len(chunks))]

        def weave(copy, c, groups):
            copy(
                woven[c][:].rearrange("p (c i t) -> p c t i", i=PACK, t=PACK)[:, groups],
                joined[:, :, chunks[c]].rearrange("p t (c i) -> p c t i", i=PACK)[:, groups],
            )

        staged = sb("staged", [P, N // P, S], F32)

        def second_product(step, c, z_codes, z_scales):
            split = step == 0
            for m in range(N // P):
                bank = psum.tile([P, CHUNK], F32, name=f"res{c}_{m}", tag=f"bank{2 * step + m}")
                nc.tensor.matmul_mx(
                    out=bank[:],
                    lhsT=w2_codes[:, m * P : (m + 1) * P].bitcast(FP8X4),
                    lhsT_scale=w2_scales[:, m * P : (m + 1) * P],
                    rhs=z_codes[:].bitcast(FP8X4),
                    rhs_scale=z_scales[:],
                    start=True,
                    stop=True,
                )
                copy = nc.vector.tensor_copy if step == 2 else nc.scalar.copy
                copy(staged[:, m, chunks[c]], bank[:])
                if split:
                    nc.sync.dma_start(out_rows[:, m, chunks[c]], staged[:, m, chunks[c]])
            if not split:
                nc.sync.dma_start(out_rows[:, :, chunks[c]], staged[:, :, chunks[c]])

        groups = CHUNK // PACK
        for c in range(len(chunks)):
            weave(nc.vector.tensor_copy if c in (1, 2) else nc.scalar.copy, c, slice(0, groups))
        order = (1, 2, 0, 3)
        z_mx = [quantise(f"z{c}", woven[c][:]) for c in order]
        for step, c in enumerate(order):
            second_product(step, c, *z_mx[step])
